import numpy as np, ml_dtypes
CORES = [6,15,38,47]
N = 4
BF = ml_dtypes.bfloat16
W, H, LG = 4096, 2048, 12
B, I, RO, A, C, DS = 16, 256, 6, 1, 1, (1,)
def pick(p, x):
    return np.take_along_axis(p, x, 3)
def swap(p, s, t):
    p = np.array(p); a = np.array(p[..., t:B * I:B])
    m = np.array(np.broadcast_to(B * np.arange(I) + (s[:, :, :1] & (B - 1)), a.shape))
    b = np.take_along_axis(p, m, 3); np.put_along_axis(p, m, a, 3); p[..., t:B * I:B] = b
    return p
def shuffled(rng):
    return rng.permuted(np.tile(np.arange(W), (N, 8, 16, 1)), axis=3)
def lanes(rng):
    return rng.integers(0, W, (N, 8, 16, I))
def join(p, s, t):
    return {"pm": (p[..., :H] + W * p[..., H:]).reshape(N, 128, H).astype(np.int32), "sa": s.reshape(N, 128, I).astype(np.int32), "ta": t.reshape(N, 128, I).astype(np.int32)}
def halves(pm):
    w = np.asarray(pm).astype(np.int64); return np.concatenate([w & (W - 1), w >> LG], axis=-1)
def setup_inputs(rng):
    return join(shuffled(rng), lanes(rng), lanes(rng))
def setup_inputs_spread(rng):
    size = np.exp2(rng.integers(0, 14, (N, 8, 16, 1)))
    p = np.argsort(np.arange(W) + size * rng.random((N, 8, 16, W)), axis=3)
    s, t = [(np.exp2(LG * rng.random((N, 8, 1, I))) * rng.random((N, 8, 16, I))).astype(np.int64) for _ in range(2)]
    return join(p, s, t)
def setup_inputs_ends(rng):
    ty = (np.arange(8)[:, None] + 1 + ((np.arange(16) + 1) % 16) // 4) % 2
    p = np.zeros((N, 8, 16, W), np.int64); end, low, n = B * (I - 1), 2 * B, len(DS)
    for v in (0, 1):
        big, small = (end, low) if v == 0 else (low, end)
        at = {big: W - 1, small: 0, end - H: W - 2 if v == 0 else 1}
        x = [W - 2 - j for j in range(n + 2)]; y = [0] + [j + 2 for j in range(n + 1)]
        at.update(zip(x, x[1:] + [big - 1])); at.update(zip(y, y[1:] + [small - 1]))
        a = np.array([c for c in at]); b = np.array([at[c] for c in at])
        ra = np.setdiff1d(np.arange(W), a); rb = np.setdiff1d(np.arange(W), b); q = np.zeros((N * int(np.count_nonzero(ty == v)), W), np.int64)
        q[:, a] = b; q[:, ra] = rng.permuted(np.tile(rb, (len(q), 1)), axis=1)
        p[:, ty == v] = q.reshape(N, -1, W)
    s = (W - 1) * rng.integers(0, 2, (N, 8, 16, I)); t = (W - 1) * rng.integers(0, 2, (N, 8, 16, I)); top = (W - 1) * (ty == 0)
    s[..., I - 1] = top; t[..., I - 1] = top; s[..., 2] = W - 1 - top; t[..., 2] = W - 1 - top
    return join(p, s, t)
def setup_inputs_corners(rng):
    p = shuffled(rng); x = np.arange(W)
    for r in range(N):
        kind = rng.permutation(8)
        for g in range(8):
            c = kind[g]
            if c == 5: p[r, g] = rng.permuted(x.reshape(W // B, B), axis=1).reshape(W)
            elif c == 6: p[r, g] = np.array(p[r, g, 0])
            elif c < 5: p[r, g] = (x, W - 1 - x, (x + 1) & (W - 1), (x - 1) & (W - 1), x ^ 1)[c]
    u = p[..., 0:B * I:B]; z = rng.integers(0, 4, (N, 8, 16, I))
    aim = np.where(z == 0, 0, np.where(z == 1, W - 1, np.where(z == 2, B * np.arange(I), lanes(rng))))
    mode = ((np.arange(N)[:, None] + np.arange(8)) % 4)[:, :, None]
    dig = np.where(mode == 0, 0, np.where(mode == 1, B - 1, np.where(mode == 2, 1, rng.integers(0, B, (N, 8, I)))))
    back = np.argsort(p[:, :, 0], axis=2)
    aim[:, :, 0] = np.take_along_axis(back, B * rng.integers(0, W // B, (N, 8, I)) + dig, 2)
    return join(p, (aim - u) & (W - 1), rng.choice(np.array([0, 1, W - 2, W - 1]), (N, 8, 16, I)))
def setup_inputs_crowd(rng):
    p = shuffled(rng); place = rng.integers(0, W, (N, 8, 16, 1)); aim = np.array(np.broadcast_to(place, (N, 8, 16, I)))
    i = int(rng.integers(0, I)); aim[:, 1::4, :, i] = (aim[:, 1::4, :, i] + 1) & (W - 1)
    aim[:, 2::4] = (W - 1) * rng.integers(0, 2, (N, 2, 16, I)); aim[:, 3::4] = place[:, 3::4, :1]
    t = np.array(np.broadcast_to(rng.integers(0, W, (N, 8, 1, 1)), (N, 8, 16, I)))
    return join(p, (aim - p[..., 0:B * I:B]) & (W - 1), t)
def setup_inputs_calm(rng):
    p = shuffled(rng); s = lanes(rng); n = W // B
    a = B * rng.permuted(np.tile(np.arange(n), (N, 8, B, 1)), axis=3) + rng.permuted(np.tile(np.arange(B), (N, 8, 1)), axis=2)[..., None]
    p[:, :, 0] = a.swapaxes(2, 3).reshape(N, 8, W)
    lone = np.arange(I) == rng.integers(0, I, (N, 8, 1))
    s[:, :, 0] = B * (s[:, :, 0] // B) + rng.integers(0, B, (N, 8, 1))
    s[:, 1::2, 0] ^= lone[:, 1::2].astype(np.int64)
    q, w, hist, back = p, s, [], []
    for t in range(RO):
        if t: w = np.roll(w, (A, C), axis=(0, 1))
        h = np.roll(q, (-A * t, -C * t), axis=(0, 1)); x = np.zeros_like(h)
        np.put_along_axis(x, h, np.broadcast_to(np.arange(W), h.shape), 3); hist.append(h); back.append(x)
        if t < RO - 1: w = pick(q, (w + q[..., t:B * I:B]) & (W - 1)); q = swap(q, w, t)
    g = np.arange(8)[:, None, None]; r = np.arange(N)[:, None, None, None]; j = (g >> 1) + 4 * r
    full = (g & 1) == 1; top = (W - 1) * (j & 1); few = (g + r) & 3
    when = np.array(np.broadcast_to(np.where(full, 1 + (j >> 1) % (RO - 1), 1 + np.arange(I) % (RO - 1)), (N, 8, 16, I)))
    want = np.where(rng.random((N, 8, 16, I)) < 0.5, few, W - 1 - (few & 1))
    for t in range(1, RO):
        e = hist[t][..., t:B * I:B]
        for v in (0, W - 1):
            m = (e == v) & ~full; when = np.where(m, t - 1, when); want = np.where(m, v, want)
    when = np.where(full & ((r & 1) == 1) & lone[:, :, None, :], RO, when)
    b = lanes(rng)
    for t in range(RO - 1, -1, -1):
        y = (pick(back[t], np.array(np.broadcast_to(top, (N, 8, 16, 1)))) - 1) & (W - 1)
        for d in DS[::-1]:
            y = pick(np.roll(back[t], -d, axis=0), y)
        y = pick(back[t], y)
        b = np.where(when == t, np.where(full, y, want), b)
        b = (pick(back[t], b) - hist[t][..., t:B * I:B]) & (W - 1)
    b[:, :, 0] = s[:, :, 0]
    w, zs = b, []
    for t in range(RO):
        w = pick(hist[t], (w + hist[t][..., t:B * I:B]) & (W - 1)); v = pick(hist[t], w)
        for d in DS:
            v = pick(np.roll(hist[t], -d, axis=0), v)
        zs.append(pick(hist[t], (v + 1) & (W - 1)))
    c = lanes(rng)
    for t in range(RO - 1, -1, -1):
        u = pick(back[t], c) - zs[t]; c = lanes(rng)
        for k in range(15, 0, -1):
            c[:, :, k] = (u[:, :, k] - c[:, :, (k + 1) & 15]) & (W - 1)
        c = np.where(full & (when == t), top, c)
    return join(p, b, np.where(full, c, rng.integers(0, 4, (N, 8, 16, I))))
def check_inputs(d):
    bad = []
    for k, lo, hi in (("pm", 1, W * W - 2), ("sa", 0, W - 1), ("ta", 0, W - 1)):
        if np.min(d[k]) < lo or np.max(d[k]) > hi: bad.append("range of " + k)
    if np.any(np.sort(halves(d["pm"]), axis=-1) != np.arange(W)): bad.append("permutations in pm")
    return bad
def reference(pm, sa, ta):
    P = halves(pm).reshape(N, 8, 16, W); S = sa.astype(np.int64).reshape(N, 8, 16, I); T = ta.astype(np.int64).reshape(N, 8, 16, I)
    for t in range(RO):
        if t:
            S = np.roll(S, (A, C), axis=(0, 1)); T = np.roll(T, (A, C), axis=(0, 1))
        S = pick(P, (S + P[..., t:B * I:B]) & (W - 1))
        z = pick(P, S)
        for a in DS:
            z = pick(np.roll(P, -a, axis=0), z)
        z = pick(P, (z + 1) & (W - 1))
        T = pick(P, (T + np.roll(T, -1, axis=2) + z) & (W - 1))
        if t < RO - 1: P = swap(P, S, t)
    return {"ys": S.reshape(N, 128, I).astype(np.float32), "yt": T.reshape(N, 128, I).astype(np.float32)}

@@ -1,0 +1,504 @@
+from concourse.mybir import AluOpType, ActivationFunctionType
+
+STEPS, LANES, WIDE, HALF = 6, 256, 4096, 2048
+NTAB = 6
+RING = 768
+NBANK = 6
+MID = 2048.0
+BIG = 51539607552.0
+CUT = 786432.0
+CUT16 = 24576.0
+
+SCRATCH = {
+    "pmi": ("sbuf", [128, HALF], "int32"),
+    "si": ("sbuf", [128, LANES], "int32"),
+    "ti": ("sbuf", [128, LANES], "int32"),
+    "hh": ("sbuf", [128, HALF], "float32"),
+    "hi": ("sbuf", [128, HALF], "int32"),
+    "gg": ("sbuf", [128, 16 * (RING + LANES)], "float16"),
+    "ones": ("sbuf", [128, 2048], "bfloat16"),
+    "dm": ("sbuf", [128, 16 + 2048], "bfloat16"),
+    "eye": ("sbuf", [128, 256], "bfloat16"),
+    "eye32": ("sbuf", [128, 128], "float32"),
+    "rot": ("sbuf", [128, 256], "bfloat16"),
+    "x1": ("sbuf", [128, 16], "int32"),
+    "x2": ("sbuf", [128, 16], "int32"),
+    "x3": ("sbuf", [128, 16], "int32"),
+    "x4": ("sbuf", [128, 16], "int32"),
+    "base": ("sbuf", [128, 16], "float32"),
+    "md": ("sbuf", [128, 16 * STEPS], "float16"),
+    "li": ("sbuf", [128, 16 * STEPS], "uint16"),
+    "yy": ("sbuf", [128, 512], "float16"),
+    "cut": ("sbuf", [128, 2 * LANES], "bfloat16"),
+    "w1": ("sbuf", [128, 2 * LANES], "int32"),
+    "w2": ("sbuf", [128, 2 * LANES], "int32"),
+    "d1": ("sbuf", [128, 16], "int32"),
+    "yo": ("sbuf", [128, 2 * LANES], "float32"),
+}
+for _n in range(NTAB):
+    SCRATCH["tab%d" % _n] = ("sbuf", [128, WIDE + 8], "float32")
+for _n in ("o1", "o2", "z1s", "o3", "z2s", "o4", "o5"):
+    SCRATCH[_n] = ("sbuf", [128, LANES * STEPS], "uint16")
+for _n in ("s16", "sl", "t16", "tl"):
+    SCRATCH[_n] = ("sbuf", [128, LANES * STEPS], "float16")
+for _n in ("m1", "m5"):
+    SCRATCH[_n] = ("sbuf", [128, LANES * STEPS], "bfloat16")
+for _n in range(8):
+    SCRATCH["ps%d" % _n] = ("psum", [128, 512], "float32")
+NMSG, NDMA = 64, 64
+SEMAPHORES = ["v", "s", "p", "g", "loc"] + ["m%d" % _n for _n in range(NMSG)] + ["d%d" % _n for _n in range(NDMA)]
+
+NOMINAL = dict(cyc=1.04, gather=1.92, scatter=4.888, pe=0.575, peo=8.0, sem=100.644, remote=4739.886, first=1983.75,
+               ghold=500.0, dma=2000.0, bw=457.96, dhold=100.0)
+ORDER = """
+10:0:4:18 10:16:24:28 10:4:8:20 10:8:16:30 10:24:32:24 00:0:0:0 20:0:16:66 20:16:32:58 30:0:16:68 11:0:16:56 30:16:32:68
+11:16:32:58 21:0:16:64 40:0:16:70 21:16:32:54 40:16:32:64 50:0:16:72 31:0:16:56 01:0:0:0 50:16:32:60 31:16:32:60
+12:0:16:66 12:16:32:60 41:0:16:68 02:0:0:0 22:0:16:62 22:16:32:66 41:16:32:62 51:0:16:68 32:0:16:62 32:16:32:54 51:16:32:62
+13:0:16:62 13:16:32:62 23:0:16:62 42:0:16:72 23:16:32:66 03:0:0:0 42:16:32:60 52:0:16:68 33:0:16:58 52:16:32:64 33:16:32:60
+14:0:16:60 14:16:32:62 43:0:16:68 24:0:16:62 04:0:0:0 24:16:32:64 43:16:32:54 53:8:16:40 53:0:8:20 34:0:16:64 34:16:32:50
+15:0:16:62 53:16:32:68 15:16:32:62 25:0:16:64 44:0:16:62 25:16:32:64 44:16:32:66 35:8:16:28 35:0:8:32 54:0:16:68 35:16:32:60
+54:16:32:64 45:8:16:36 45:0:8:46 45:24:32:34 45:16:24:36 55:8:16:26 55:0:8:36 55:24:32:40 55:16:24:26
+"""
+TUNE = dict(
+    seq=[(int(x[0][0]), int(x[0][1]), 8 * int(x[1]), 8 * int(x[2]), int(x[3])) for x in [w.split(":") for w in ORDER.split()]],
+    loads=[(0, 256), (256, 512), (512, 1024), (1024, 1536), (1536, 2048)],
+    pieces=[(0, 256), (256, 512), (512, 1024), (1024, 1536), (1536, 1792), (1792, 2048)],
+    behind={("sl", False): 768, ("o3", False): 2048, "now": 1024, ("tl", True): 2048, ("o4", False): 2048},
+    md="tt", mod1="tt", mod5="tt", m1="s", m5="s", plain=None, bg="s", turn={}, gcopy=0, margin=250.0, ahead=100.0)
+
+
+def units(name, t, a, b, w=8):
+    return [(name, t, u) for u in range(a // w, (b + w - 1) // w)]
+
+
+def make_ops(tune):
+    A, AF = AluOpType, ActivationFunctionType
+    ops, wrote, read = [], {}, {}
+    count = dict(msg=0, dma=0, ring=0, bank=0, turn=0, copy=(0, WIDE))
+    count["int"] = 0
+    plain = tune["plain"] is not None
+
+    def add(eng, cost, r, w, emit, fixed=False, sem=None, to=0):
+        deps = set()
+        for x in r:
+            if x in wrote:
+                deps.add(wrote[x])
+        for x in w:
+            if x in wrote:
+                deps.add(wrote[x])
+            deps.update(read.get(x, ()))
+        if eng == "p":
+            deps = {d for d in deps if ops[d]["eng"] != "p"}
+        me = len(ops)
+        for x in r:
+            read.setdefault(x, []).append(me)
+        for x in w:
+            wrote[x] = me
+            read[x] = []
+        ops.append(dict(eng=eng, cost=cost, deps=sorted(deps), emit=emit, fixed=fixed, sem=sem, to=to))
+
+    def dma(eng, nbytes, r, w, emit, fixed=False):
+        add(eng, ("dma", nbytes), r, w, emit, fixed=fixed, sem="d%d" % count["dma"])
+        count["dma"] += 1
+
+    def send(to, src, dst, t, u, a, b):
+        add("g", ("remote", 0), units(src, t, a, b), units(dst, u, a, b),
+            lambda T: (T[dst][:, LANES * u + a:LANES * u + b], T[src][:, LANES * t + a:LANES * t + b]),
+            sem="m%d" % count["msg"], to=to)
+        count["msg"] += 1
+        more(tune["behind"].get((dst, b == LANES), 0), units(dst, u, a, b))
+
+    def more(n, behind):
+        t, a = count["copy"]
+        b = min(a + n, WIDE)
+        if b > a:
+            copy(t, a, b, behind)
+            count["copy"] = (t, b)
+
+    def lane(T, name, t, a, b):
+        return T[name][:, LANES * t + a:LANES * t + b]
+
+    def tabs(t, a=0, b=WIDE):
+        return units("tab", t % NTAB, a, b, 256)
+
+    def tab(T, t):
+        return T["tab%d" % (t % NTAB)]
+
+    def bank():
+        count["bank"] += 1
+        return "ps%d" % ((count["bank"] - 1) % NBANK)
+
+    for n, (a, b) in enumerate(tune["loads"]):
+        dma("y" if n % 2 == 0 else "s", 512 * (b - a), [], units("pm", 0, a, b, 128),
+            lambda q, T, a=a, b=b: q.dma_start(T.pmi[:, a:b], T.pm[:, a:b]), fixed=True)
+        if n == 2:
+            dma("y", 512 * LANES, [], ["si"], lambda q, T: q.dma_start(T.si[:], T.sa[:]), fixed=True)
+    dma("y", 512 * LANES, [], ["ti"], lambda q, T: q.dma_start(T.ti[:], T.ta[:]), fixed=True)
+    add("v", ("el", 1024), [], ["ones"], lambda q, T: q.memset(T.ones[:], 1.0))
+    add("v", ("el", 16), [], ["pad"], lambda q, T: q.memset(T.dm[:, 0:16], 0.0))
+    add("v", ("el", 128), [], ["cut"], lambda q, T: q.memset(T.cut[0:32, 0:LANES], CUT / 32))
+    add("v", ("el", 128), ["cut"], ["cut"], lambda q, T: q.memset(T.cut[32:64, 0:LANES], MID / 32))
+    add("v", ("el", 16), ["cut"], ["cut"], lambda q, T: q.memset(T.cut[0:32, LANES:LANES + 16], CUT16 / 32))
+    add("g", ("gp", 16), [], ["x1"], lambda q, T: q.iota(T.x1[:], [[0, 16]], 0, 16))
+    add("g", ("gp", 16), [], ["x2"], lambda q, T: q.iota(T.x2[:], [[256, 16]], 0, 0))
+    add("g", ("gp", 256), ["ones"], ["eye"],
+        lambda q, T: q.affine_select(T.eye[:], T.ones[:, 0:256], [[0, 2], [-1, 128]], A.is_equal, 0.0, 0, 1))
+    add("g", ("gp", 2048), ["ones"], ["dm"],
+        lambda q, T: q.affine_select(T.dm[:, 16:2064], T.ones[:], [[-1, 16], [-512, 8], [-31, 16]], A.is_equal, 0.0, 0, 32))
+    add("v", ("el", 16), ["x1"], ["x3"], lambda q, T: q.tensor_scalar(T.x3[:], T.x1[:], 255, None, A.bitwise_and))
+    add("v", ("el", 32), ["x3", "x2"], ["x4"], lambda q, T: q.tensor_tensor(T.x4[:], T.x3[:], T.x2[:], A.add))
+    add("v", ("el", 16), ["x4"], ["base"], lambda q, T: q.tensor_scalar(T.base[:], T.x4[:], 7.5, None, A.add))
+    add("s", ("el", 128), ["eye"], ["eye32"], lambda q, T: q.activation(T.eye32[:], T.eye[:, 0:128], AF.Copy))
+    add("s", ("el", 255), ["eye"], ["rot"], lambda q, T: q.activation(T.rot[:, 0:255], T.eye[:, 1:256], AF.Copy))
+    add("s", ("el", 16), ["eye"], ["rot"], lambda q, T: q.activation(T.rot[:, 15:256:16], T.eye[:, 0:256:16], AF.Copy))
+    add("v", ("el", LANES), ["si"], units("sl", 0, 0, LANES),
+        lambda q, T: q.tensor_scalar(lane(T, "sl", 0, 0, LANES), T.si[:], -MID, None, A.add))
+
+    def index1(t, a, b, ps):
+        n, o = b - a, 112 if t else 0
+
+        how = tune["mod1"]
+
+        def sums(q, T, extra):
+            q.matmul(T[ps][:, 0:n], T.eye[:, o:o + 128], lane(T, "sl", t, a, b), True, False)
+            if how == "tt":
+                rows = 64 if plain else 32
+                q.matmul(T[ps][:, 0:n], T.ones[0:rows, 0:128], T.cut[0:rows, 0:n], False, False)
+            elif extra is not None:
+                q.matmul(T[ps][:, 0:n], T.eye[:, 0:128], extra, False, False)
+            return q.matmul(T[ps][:, 0:n], T.eye32[:], tab(T, t)[:, 16 * a + t:16 * b:16], False, True)
+        r = ["eye", "eye32"] + units("sl", t, a, b) + tabs(t, 16 * a, 16 * b)
+        if how == "tt":
+            add("p", ("mm", [n, n, max(n, 64) * 4]), r + ["cut", "ones"], [ps], lambda q, T: sums(q, T, None))
+        else:
+            add("p", ("mm", [n, max(n, 64) * 4]), r, [ps], lambda q, T: sums(q, T, None))
+        if how == "again":
+            add("s", ("el", n), [], [ps, ("m1", t, a)],
+                lambda q, T: q.activation(lane(T, "m1", t, a, b), T[ps][:, 0:n], AF.Identity, bias=-(CUT - 2047.5), scale=-1.0))
+            add("p", ("mm", [n, n, max(n, 64) * 4]), r + [("m1", t, a)], [ps], lambda q, T: sums(q, T, lane(T, "m1", t, a, b)))
+            add("v", ("el", n), [], [ps] + units("o1", t, a, b),
+                lambda q, T: q.tensor_scalar(lane(T, "o1", t, a, b), T[ps][:, 0:n], CUT, None, A.add))
+        else:
+            remainder(how, ps, "o1", "m1", t, a, b, 2 * MID)
+
+    def remainder(how, ps, name, tmp, t, a, b, plus):
+        n = b - a
+        if how == "tt":
+            if tune[tmp] == "s":
+                add("s", ("el", n), [], [ps, (tmp, t, a)],
+                    lambda q, T: q.activation(lane(T, tmp, t, a, b), T[ps][:, 0:n], AF.Identity, bias=2047.5, scale=-1.0))
+            else:
+                add("v", ("el", n), [], [ps, (tmp, t, a)],
+                    lambda q, T: q.tensor_scalar(lane(T, tmp, t, a, b), T[ps][:, 0:n], -1.0, 2047.5, A.mult, A.add))
+            add("v", ("el", n), [(tmp, t, a)], [ps] + units(name, t, a, b),
+                lambda q, T: q.tensor_tensor(lane(T, name, t, a, b), T[ps][:, 0:n], lane(T, tmp, t, a, b), A.add))
+        else:
+            w = 256 * (count["int"] % 2)
+            count["int"] += 1
+            add("v", ("el", n), [], [ps, ("w1", w)], lambda q, T: q.tensor_scalar(T.w1[:, w:w + n], T[ps][:, 0:n], plus, None, A.add))
+            add("v", ("el", n), [("w1", w)], [("w2", w)],
+                lambda q, T: q.tensor_scalar(T.w2[:, w:w + n], T.w1[:, w:w + n], WIDE - 1, None, A.bitwise_and))
+            add("v", ("el", n), [("w2", w)], units(name, t, a, b), lambda q, T: q.tensor_copy(lane(T, name, t, a, b), T.w2[:, w:w + n]))
+
+    def last_column(t):
+        dma("y", 8192, tabs(t, 0, 1), [("end", t % NTAB)], lambda q, T: q.dma_start(tab(T, t)[:, WIDE:WIDE + 1], tab(T, t)[:, 0:1]))
+
+    def copy(t, a, b, behind):
+        dma("y", 512 * (b - a), tabs(t, a, b) + behind, tabs(t + 1, a, b),
+            lambda q, T: q.dma_start(tab(T, t + 1)[:, a:b], tab(T, t)[:, a:b]))
+
+    for a, b in tune["pieces"]:
+        n, ps = b - a, bank()
+        pmr = units("pm", 0, a, b, 128)
+        if plain:
+            add("v", ("el", n), pmr, tabs(0, a, b),
+                lambda q, T, a=a, b=b: q.tensor_scalar(T.tab0[:, a:b], T.pmi[:, a:b], WIDE - 1, None, A.bitwise_and))
+            if a in tune["plain"]:
+                add("v", ("el", n), pmr, tabs(0, HALF + a, HALF + b),
+                    lambda q, T, a=a, b=b: q.tensor_scalar(T.tab0[:, HALF + a:HALF + b], T.pmi[:, a:b], 12, None, A.logical_shift_right))
+            else:
+                add("s", ("el", n), pmr, [("hh", a)],
+                    lambda q, T, a=a, b=b: q.activation(T.hi[:, a:b], T.pmi[:, a:b], AF.Identity,
+                                                        bias=-(2047.0 + 2047.5 / WIDE), scale=1.0 / WIDE))
+                add("s", ("el", n), [("hh", a)], tabs(0, HALF + a, HALF + b),
+                    lambda q, T, a=a, b=b: q.activation(T.tab0[:, HALF + a:HALF + b], T.hi[:, a:b], AF.Identity, bias=2047.0))
+        else:
+            add("v", ("el", n), pmr, [("hh", a)],
+                lambda q, T, a=a, b=b: q.tensor_scalar(T.hh[:, a:b], T.pmi[:, a:b], -8386559.5, BIG, A.add, A.add))
+            add("s", ("el", n), [("hh", a)], tabs(0, HALF + a, HALF + b),
+                lambda q, T, a=a, b=b: q.activation(T.tab0[:, HALF + a:HALF + b], T.hh[:, a:b], AF.Identity,
+                                                    bias=-(BIG / WIDE + 1.0), scale=1.0 / WIDE))
+            add("s", ("el", n), tabs(0, HALF + a, HALF + b), [ps],
+                lambda q, T, a=a, b=b, ps=ps: q.activation(T[ps][:, 0:b - a], T.tab0[:, HALF + a:HALF + b], AF.Identity,
+                                                           bias=WIDE * MID + MID, scale=float(WIDE)))
+            add("v", ("el", n), pmr, [ps] + tabs(0, a, b),
+                lambda q, T, a=a, b=b, ps=ps: q.tensor_tensor(T.tab0[:, a:b], T.pmi[:, a:b], T[ps][:, 0:b - a], A.subtract))
+        if b in (1024, 2048):
+            index1(0, b // 16 + 64, b // 16 + 128, "ps6")
+            index1(0, b // 16 - 64, b // 16, "ps7")
+            copy(0, HALF + b - 1024, HALF + b, [])
+            copy(0, b - 1024, b, [])
+    last_column(0)
+
+    done = {}
+
+    def gather(k, t, a, b, c):
+        last = t == STEPS - 1
+        n = b - a
+        if k == 1:
+            r0 = RING + a
+        else:
+            if count["ring"] + n > RING:
+                count["ring"] = 0
+            r0 = count["ring"]
+            count["ring"] += n
+        s0 = 16 * r0
+        off, wide = "o%d" % k, WIDE + 1 if k == 4 else WIDE
+        tr = tabs(t) + ([("end", t % NTAB)] if k == 4 else [])
+
+        def by_vector(q, T):
+            out, win = T.gg[:, s0:s0 + 16 * (c - a)], tab(T, t)[:, 0:wide].indirect(lane(T, off, t, a, c))
+            return q.tensor_scalar(out, win, -MID, None, A.add) if plain else q.tensor_copy(out, win)
+
+        def by_scalar(q, T):
+            out, win = T.gg[:, s0 + 16 * (c - a):s0 + 16 * n], tab(T, t)[:, 0:wide].indirect(lane(T, off, t, c, b))
+            return q.activation(out, win, AF.Identity, bias=-MID) if plain else q.activation(out, win, AF.Copy)
+        add("v", ("gather", 16 * (c - a)), tr + units(off, t, a, c), units("gg", 0, r0, r0 + c - a, 2), by_vector, fixed=True)
+        add("s", ("gather", 16 * (b - c)), tr + units(off, t, c, b), units("gg", 0, r0 + c - a, r0 + n, 2), by_scalar, fixed=True)
+        ps, o = bank(), 112 if t else 0
+        turned = k in tune["turn"] and n <= 128
+        if turned:
+            p0, y0 = bank(), 128 * (count["turn"] % 4)
+            count["turn"] += 1
+
+            def turn(q, T):
+                for j in range(16):
+                    m = q.matmul(T[p0][0:n, j:128:16], T.gg[:, s0 + j:s0 + 16 * n:16], T.eye[:, j:128:16], True, True)
+                return m
+            add("p", ("mm", [8] * 16), ["eye"] + units("gg", 0, r0, r0 + n, 2), [p0], turn)
+            if tune["turn"][k] == "s":
+                add("s", ("el", 128), [], [p0, ("yy", y0)], lambda q, T: q.activation(T.yy[0:n, y0:y0 + 128], T[p0][0:n, 0:128], AF.Copy))
+            else:
+                add("v", ("el", 128), [], [p0, ("yy", y0)], lambda q, T: q.tensor_copy(T.yy[0:n, y0:y0 + 128], T[p0][0:n, 0:128]))
+
+        def pick(q, T):
+            if turned:
+                m = q.matmul(T[ps][:, 0:n], T.yy[0:n, y0:y0 + 128], T.eye[0:n, 0:n], True, k != 4)
+            else:
+                for j in range(16):
+                    m = q.matmul(T[ps][:, 0:n], T.dm[:, 16 + 128 * j:144 + 128 * j], T.gg[:, s0 + j:s0 + 16 * n:16],
+                                 j == 0, j == 15 and k != 4)
+            if k == 4:
+                if tune["mod5"] == "tt":
+                    q.matmul(T[ps][:, 0:n], T.ones[0:64, 0:128], T.cut[0:64, 0:n], False, False)
+                q.matmul(T[ps][:, 0:n], T.eye[:, o:o + 128], lane(T, "tl", t, a, b), False, False)
+                m = q.matmul(T[ps][:, 0:n], T.rot[:, o:o + 128], lane(T, "tl", t, a, b), False, True)
+            return m
+        r = ["eye", ("yy", y0)] if turned else ["dm"] + units("gg", 0, r0, r0 + n, 2)
+        r += ["eye", "rot", "cut", "ones"] + units("tl", t, a, b) if k == 4 else []
+        add("p", ("mm", [n] * ((1 if turned else 16) + ((3 if tune["mod5"] == "tt" else 2) if k == 4 else 0))), r, [ps], pick)
+
+        def offsets(name, plus):
+            add("v", ("el", n), [], [ps] + units(name, t, a, b),
+                lambda q, T: q.tensor_scalar(lane(T, name, t, a, b), T[ps][:, 0:n], plus, None, A.add))
+
+        def keep(name, col):
+            if last:
+                add("s", ("el", n), [], [ps] + units(name, t, a, b),
+                    lambda q, T: q.activation(T.yo[:, col + a:col + b], T[ps][:, 0:n], AF.Identity, bias=MID))
+            else:
+                add("s", ("el", n), [], [ps] + units(name, t, a, b),
+                    lambda q, T: q.activation(lane(T, name, t, a, b), T[ps][:, 0:n], AF.Copy))
+        done[(k, t)] = done.get((k, t), 0) + n
+        whole = done[(k, t)] == LANES
+        if k == 1:
+            offsets("o2", MID)
+            keep("s16", 0)
+            if whole and last:
+                dma("y", 512 * LANES, units("s16", t, 0, LANES), [], lambda q, T: q.dma_start(T.ys[:], T.yo[:, 0:LANES]))
+            elif t == 0 and a == 0:
+                send(1, "s16", "sl", t, t + 1, a, b)
+                done["early"] = b
+            if whole and not last:
+                send(1, "s16", "sl", t, t + 1, done.pop("early", 0), LANES)
+                places(t)
+        elif k == 2:
+            offsets("z1s", MID)
+            send(1, "z1s", "o3", t, t, a, b)
+        elif k == 3:
+            offsets("z2s", MID + 1.0)
+            send(-1, "z2s", "o4", t, t, a, b)
+        elif k == 4:
+            remainder(tune["mod5"], ps, "o5", "m5", t, a, b, 3 * MID)
+        else:
+            keep("t16", LANES)
+            if last:
+                dma("y", 512 * n, units("t16", t, a, b), [],
+                    lambda q, T: q.dma_start(T.yt[:, a:b], T.yo[:, LANES + a:LANES + b]))
+            elif t == STEPS - 2:
+                send(1, "t16", "tl", t, t + 1, a, b)
+            elif whole:
+                send(1, "t16", "tl", t, t + 1, 0, LANES)
+
+    def places(t):
+        def spread(q, T):
+            for j in range(16):
+                q.matmul(T.ps7[:, 0:16], T.dm[:, 16 - j:144 - j], T.gg[:, 16 * (RING + j):16 * (RING + LANES):256], j == 0, False)
+            return q.matmul(T.ps7[:, 0:16], T.ones[0:32, 0:128], T.cut[0:32, LANES:LANES + 16], False, True)
+        add("p", ("mm", [16] * 17), ["dm", "pad", "ones", "cut"] + units("gg", 0, RING, RING + LANES, 2), ["ps7"], spread)
+        add("v", ("el", 16), ["base"], ["ps7", ("md", t)],
+            lambda q, T: q.tensor_tensor(T.md[:, 16 * t:16 * t + 16], T.base[:], T.ps7[:, 0:16], A.subtract))
+        if tune["md"] == "tt":
+            add("v", ("el", 16), [("md", t)], ["ps7", ("li", t)],
+                lambda q, T: q.tensor_tensor(T.li[:, 16 * t:16 * t + 16], T.ps7[:, 0:16], T.md[:, 16 * t:16 * t + 16], A.add))
+        else:
+            add("v", ("el", 16), [("md", t)], ["ps7", "d1"],
+                lambda q, T: q.tensor_tensor(T.d1[:], T.ps7[:, 0:16], T.md[:, 16 * t:16 * t + 16], A.add))
+            add("v", ("el", 16), ["d1"], [("li", t)], lambda q, T: q.tensor_copy(T.li[:, 16 * t:16 * t + 16], T.d1[:]))
+
+    def swap(t):
+        more(WIDE, [])
+        if tune["bg"] == "s":
+            add("s", ("gather", LANES), tabs(t) + [("li", t)], tabs(t + 1),
+                lambda q, T: q.activation(tab(T, t + 1)[:, t:WIDE:16], tab(T, t)[:, 0:WIDE].indirect(T.li[:, 16 * t:16 * t + 16]), AF.Copy))
+        else:
+            add("v", ("gather", LANES), tabs(t) + [("li", t)], tabs(t + 1),
+                lambda q, T: q.tensor_copy(tab(T, t + 1)[:, t:WIDE:16], tab(T, t)[:, 0:WIDE].indirect(T.li[:, 16 * t:16 * t + 16])))
+        add("v", ("scatter", LANES), tabs(t) + [("li", t)], tabs(t + 1),
+            lambda q, T: q.tensor_copy(tab(T, t + 1)[:, 0:WIDE].indirect(T.li[:, 16 * t:16 * t + 16]), tab(T, t)[:, t:WIDE:16]))
+        if t == 0:
+            add("v", ("el", LANES), ["ti", ("li", 0)], units("tl", 0, 0, LANES),
+                lambda q, T: q.tensor_scalar(lane(T, "tl", 0, 0, LANES), T.ti[:], -MID, None, A.add))
+        last_column(t + 1)
+        index1(t + 1, 0, LANES, "ps6")
+        if t < STEPS - 2:
+            for a in range(0, tune["gcopy"], 512):
+                add("g", ("gp", 512), tabs(t + 1, a, a + 512), tabs(t + 2, a, a + 512),
+                    lambda q, T, a=a: q.affine_select(tab(T, t + 2)[:, a:a + 512], tab(T, t + 1)[:, a:a + 512], [[0, 512]],
+                                                      A.is_ge, 0.0, 0, 0))
+            count["copy"] = (t + 1, tune["gcopy"])
+            more(tune["behind"].get("now", 0), [])
+
+    for k, t, a, b, v in tune["seq"]:
+        if k:
+            gather(k, t, a, b, a + v)
+        else:
+            swap(t)
+    return ops
+
+
+def spans(op, M, state, start):
+    kind, n = op["cost"]
+    if kind == "dma":
+        at = max(start + M["dma"] / 2, state.get("dma", 0.0)) + n / M["bw"]
+        state["dma"] = at
+        return start + M["dhold"], at + M["dma"] / 2
+    if kind == "remote":
+        extra = 0.0 if state.get("sent") else M["first"]
+        state["sent"] = True
+        at = max(start + extra + M["remote"] / 3, state.get("dma", 0.0)) + M["remote"] / 3
+        state["dma"] = at
+        return start + M["ghold"] + extra, at + M["remote"] / 3
+    if kind == "mm":
+        d = sum(max(64, x) * M["pe"] + M["peo"] for x in n)
+    elif kind == "gp":
+        d = 170.0 + 2 * n * M["cyc"]
+    else:
+        rate = 1.0 if kind == "el" else M[kind]
+        d = (50.0 if op["eng"] == "v" else 65.0) + max(64, n * rate) * M["cyc"]
+    return start + d, start + d
+
+
+def order_ops(ops, tune, M):
+    n = len(ops)
+    left = [len(o["deps"]) for o in ops]
+    after = [[] for _ in ops]
+    for i, o in enumerate(ops):
+        for d in o["deps"]:
+            after[d].append(i)
+    chain = {e: [i for i in range(n) if ops[i]["eng"] == e and ops[i]["fixed"]] for e in "vspgy"}
+    head = {e: 0 for e in chain}
+    free = {e: 0.0 for e in chain}
+    end, state, order = [0.0] * n, {}, []
+    due = {i: 0.0 for i in range(n) if not left[i]}
+    while due:
+        best = None
+        for i, r in due.items():
+            o = ops[i]
+            e = o["eng"]
+            if o["fixed"] and chain[e][head[e]] != i:
+                continue
+            s = max(free[e], r)
+            key = (s + (tune["ahead"] if o["fixed"] and o["cost"][0] == "gather" else 0.0), i)
+            if best is None or key < best[0]:
+                best = (key, i, s)
+        _, i, s = best
+        e = ops[i]["eng"]
+        free[e], end[i] = spans(ops[i], M, state, s)
+        if ops[i]["fixed"]:
+            head[e] += 1
+        order.append(i)
+        del due[i]
+        for j in after[i]:
+            left[j] -= 1
+            if not left[j]:
+                o = ops[j]
+                loose = not o["fixed"] and o["eng"] in "vs"
+                due[j] = max(end[d] + M["sem"] + (tune["margin"] if loose and ops[d]["eng"] != o["eng"] else 0.0) for d in o["deps"])
+    return order
+
+
+PLAN = {}
+
+
+def plan():
+    if not PLAN:
+        ops = make_ops(TUNE)
+        PLAN["ops"], PLAN["order"] = ops, order_ops(ops, TUNE, NOMINAL)
+    return PLAN["ops"], PLAN["order"]
+
+
+def rank_program(g, core, T, topo):
+    rank = T.rank_of(core)
+    if rank is None:
+        return
+    ops, order = plan()
+    queue = {"v": g.vector, "s": g.scalar, "p": g.tensor, "g": g, "y": g.sync}
+    peer = {}
+    for to in (1, -1):
+        other = T.cores[(rank + to) % len(T.cores)]
+        rid, pid, _ = topo.addr(other)
+        peer[to] = (pid, rid, topo.mask(core, other), len(topo.engines(core, other)),
+                    len(topo.engines(T.cores[(rank - to) % len(T.cores)], core)))
+    mark, know, total = {}, {e: {} for e in queue}, {}
+    for i in order:
+        o = ops[i]
+        e, q = o["eng"], queue[o["eng"]]
+        need = {}
+        for d in o["deps"]:
+            s, val, _ = mark[d]
+            if need.get(s, (0, None))[0] < val:
+                need[s] = (val, d)
+        for s, (val, d) in sorted(need.items(), key=lambda x: -x[1][1]):
+            if know[e].get(s, 0) < val:
+                q.wait_ge(T.sem[s], val)
+                know[e][s] = val
+                for s2, v2 in mark[d][2].items():
+                    know[e][s2] = max(know[e].get(s2, 0), v2)
+        if o["to"]:
+            pid, rid, mask, sent, comes = peer[o["to"]]
+            out, src = o["emit"](T)
+            g.remote_dma(out, src, T.sem[o["sem"]], T.sem.loc, pid, rid, mask)
+            total["loc"] = total.get("loc", 0) + sent
+            mark[i] = (o["sem"], comes, {})
+        elif o["sem"]:
+            o["emit"](q, T).then_inc(T.sem[o["sem"]], 16)
+            total[o["sem"]] = 16
+            mark[i] = (o["sem"], 16, dict(know[e]))
+        else:
+            o["emit"](q, T).then_inc(T.sem[e], 1)
+            total[e] = total.get(e, 0) + 1
+            mark[i] = (e, total[e], dict(know[e]))
+    for s, val in total.items():
+        if know["y"].get(s, 0) < val:
+            g.sync.wait_ge(T.sem[s], val)

@@ -1,26 +1,30 @@
 from concourse.mybir import AluOpType, ActivationFunctionType
 
 STEPS, LANES, WIDE, HALF = 6, 256, 4096, 2048
-NTAB = 6
-RING = 768
+NG = 5
 NBANK = 6
 MID = 2048.0
 BIG = 51539607552.0
 CUT = 786432.0
 CUT16 = 24576.0
+SUMS = [(MID - 0.5, 65), (BIG, 32), (-BIG, 32), (CUT + MID, 40), (CUT16, 32), (-0.5, 32)]
+SW = 144
 
 SCRATCH = {
     "pmi": ("sbuf", [128, HALF], "int32"),
     "si": ("sbuf", [128, LANES], "int32"),
     "ti": ("sbuf", [128, LANES], "int32"),
-    "hh": ("sbuf", [128, HALF], "float32"),
     "hi": ("sbuf", [128, HALF], "int32"),
-    "gg": ("sbuf", [128, 16 * (RING + LANES)], "float16"),
+    "gg": ("sbuf", [128, WIDE * NG], "float16"),
     "ones": ("sbuf", [128, 2048], "bfloat16"),
     "dm": ("sbuf", [128, 16 + 2048], "bfloat16"),
     "eye": ("sbuf", [128, 256], "bfloat16"),
-    "eye32": ("sbuf", [128, 128], "float32"),
+    "neg": ("sbuf", [128, 256], "bfloat16"),
     "rot": ("sbuf", [128, 256], "bfloat16"),
+    "eye32": ("sbuf", [128, 384], "float32"),
+    "cut": ("sbuf", [128, 128 * len(SUMS)], "bfloat16"),
+    "pw": ("sbuf", [128, LANES * STEPS], "float32"),
+    "tw": ("sbuf", [128, LANES], "float32"),
     "x1": ("sbuf", [128, 16], "int32"),
     "x2": ("sbuf", [128, 16], "int32"),
     "x3": ("sbuf", [128, 16], "int32"),
@@ -28,43 +32,37 @@ SCRATCH = {
     "base": ("sbuf", [128, 16], "float32"),
     "md": ("sbuf", [128, 16 * STEPS], "float16"),
     "li": ("sbuf", [128, 16 * STEPS], "uint16"),
-    "yy": ("sbuf", [128, 512], "float16"),
-    "cut": ("sbuf", [128, 2 * LANES], "bfloat16"),
-    "w1": ("sbuf", [128, 2 * LANES], "int32"),
-    "w2": ("sbuf", [128, 2 * LANES], "int32"),
-    "d1": ("sbuf", [128, 16], "int32"),
     "yo": ("sbuf", [128, 2 * LANES], "float32"),
+    "m5": ("sbuf", [128, LANES * STEPS], "bfloat16"),
 }
-for _n in range(NTAB):
-    SCRATCH["tab%d" % _n] = ("sbuf", [128, WIDE + 8], "float32")
+for _n in range(STEPS):
+    SCRATCH["tab%d" % _n] = ("sbuf", [128, WIDE + 8], "int32")
 for _n in ("o1", "o2", "z1s", "o3", "z2s", "o4", "o5"):
     SCRATCH[_n] = ("sbuf", [128, LANES * STEPS], "uint16")
-for _n in ("s16", "sl", "t16", "tl"):
+for _n in ("s16", "sl", "t16", "tl", "pn"):
     SCRATCH[_n] = ("sbuf", [128, LANES * STEPS], "float16")
-for _n in ("m1", "m5"):
-    SCRATCH[_n] = ("sbuf", [128, LANES * STEPS], "bfloat16")
-for _n in range(8):
+for _n in ("su", "sv"):
+    SCRATCH[_n] = ("sbuf", [128, 2 * SW * STEPS], "float16")
+for _n in range(NBANK + 1):
     SCRATCH["ps%d" % _n] = ("psum", [128, 512], "float32")
-NMSG, NDMA = 64, 64
-SEMAPHORES = ["v", "s", "p", "g", "loc"] + ["m%d" % _n for _n in range(NMSG)] + ["d%d" % _n for _n in range(NDMA)]
+NMSG, NDMA = 50, 46
+SEMAPHORES = ["v", "s", "p", "g"] + [_x % _n for _x in ("m%d", "lm%d") for _n in range(NMSG)] + ["d%d" % _n for _n in range(NDMA)]
 
-NOMINAL = dict(cyc=1.04, gather=1.92, scatter=4.888, pe=0.575, peo=8.0, sem=100.644, remote=4739.886, first=1983.75,
-               ghold=500.0, dma=2000.0, bw=457.96, dhold=100.0)
-ORDER = """
-10:0:4:18 10:16:24:28 10:4:8:20 10:8:16:30 10:24:32:24 00:0:0:0 20:0:16:66 20:16:32:58 30:0:16:68 11:0:16:56 30:16:32:68
-11:16:32:58 21:0:16:64 40:0:16:70 21:16:32:54 40:16:32:64 50:0:16:72 31:0:16:56 01:0:0:0 50:16:32:60 31:16:32:60
-12:0:16:66 12:16:32:60 41:0:16:68 02:0:0:0 22:0:16:62 22:16:32:66 41:16:32:62 51:0:16:68 32:0:16:62 32:16:32:54 51:16:32:62
-13:0:16:62 13:16:32:62 23:0:16:62 42:0:16:72 23:16:32:66 03:0:0:0 42:16:32:60 52:0:16:68 33:0:16:58 52:16:32:64 33:16:32:60
-14:0:16:60 14:16:32:62 43:0:16:68 24:0:16:62 04:0:0:0 24:16:32:64 43:16:32:54 53:8:16:40 53:0:8:20 34:0:16:64 34:16:32:50
-15:0:16:62 53:16:32:68 15:16:32:62 25:0:16:64 44:0:16:62 25:16:32:64 44:16:32:66 35:8:16:28 35:0:8:32 54:0:16:68 35:16:32:60
-54:16:32:64 45:8:16:36 45:0:8:46 45:24:32:34 45:16:24:36 55:8:16:26 55:0:8:36 55:24:32:40 55:16:24:26
-"""
+NOMINAL = dict(cyc=0.96, gather=1.45, scatter=3.6, pe=0.55, peo=8.0, sem=80.0, remote=2600.0, first=2000.0,
+               ghold=300.0, dma=1300.0, bw=280.0, dhold=100.0, link=50.0)
+CHUNKS = {"W": [(0, 256)], "H": [(0, 128), (128, 256)], "A": [(0, 64), (128, 192), (64, 128), (192, 256)],
+          "Y": [(0, 128), (128, 192), (192, 256)], "-": []}
+ORDER = """10A 00- 20H 11H 01- 30H 21W  12W 40W 31W 22W 02- 50W  13W 41W 32W 23W 03- 51W  14W 42W 33W 24W 52W 04-
+           15W 43W 34W 25H 53H  44H 35H 54H 45H 55Y"""
+
 TUNE = dict(
-    seq=[(int(x[0][0]), int(x[0][1]), 8 * int(x[1]), 8 * int(x[2]), int(x[3])) for x in [w.split(":") for w in ORDER.split()]],
-    loads=[(0, 256), (256, 512), (512, 1024), (1024, 1536), (1536, 2048)],
-    pieces=[(0, 256), (256, 512), (512, 1024), (1024, 1536), (1536, 1792), (1792, 2048)],
-    behind={("sl", False): 768, ("o3", False): 2048, "now": 1024, ("tl", True): 2048, ("o4", False): 2048},
-    md="tt", mod1="tt", mod5="tt", m1="s", m5="s", plain=None, bg="s", turn={}, gcopy=0, margin=250.0, ahead=100.0)
+    seq=[(int(_w[0]), int(_w[1]), CHUNKS[_w[2]]) for _w in ORDER.split()],
+    loads=[(0, 256), (256, 1024), (1024, 1792), (1792, 2048)], sa=2,
+    pieces=[(0, 256, 0), (256, 1024, 256), (1024, 1792, 256), (1792, 2048, 128)],
+    turn_s=(1, 2, 3, 4), wide=(3, 4, 5), on_s=("z1s",),
+    pools=[0, 1024, 3072, 2048, 2048, 2048], pool=768,
+    now=[1024, 512, 2048, 2048], behind=512,
+    margin=300.0, ahead=300.0, skew=-50.0, rounds=2, damp=0.5)
 
 
 def units(name, t, a, b, w=8):
@@ -73,10 +71,8 @@ def units(name, t, a, b, w=8):
 
 def make_ops(tune):
     A, AF = AluOpType, ActivationFunctionType
-    ops, wrote, read = [], {}, {}
-    count = dict(msg=0, dma=0, ring=0, bank=0, turn=0, copy=(0, WIDE))
-    count["int"] = 0
-    plain = tune["plain"] is not None
+    ops, wrote, read, pairs = [], {}, {}, []
+    count = dict(msg=0, dma=0, tile=0, bank=0, copy=(-1, WIDE), stop=WIDE)
 
     def add(eng, cost, r, w, emit, fixed=False, sem=None, to=0):
         deps = set()
@@ -87,8 +83,6 @@ def make_ops(tune):
             if x in wrote:
                 deps.add(wrote[x])
             deps.update(read.get(x, ()))
-        if eng == "p":
-            deps = {d for d in deps if ops[d]["eng"] != "p"}
         me = len(ops)
         for x in r:
             read.setdefault(x, []).append(me)
@@ -96,356 +90,389 @@ def make_ops(tune):
             wrote[x] = me
             read[x] = []
         ops.append(dict(eng=eng, cost=cost, deps=sorted(deps), emit=emit, fixed=fixed, sem=sem, to=to))
+        return me
 
-    def dma(eng, nbytes, r, w, emit, fixed=False):
-        add(eng, ("dma", nbytes), r, w, emit, fixed=fixed, sem="d%d" % count["dma"])
+    def dma(nbytes, r, w, emit):
+        add("y", ("dma", nbytes), r, w, emit, sem="d%d" % count["dma"])
         count["dma"] += 1
 
-    def send(to, src, dst, t, u, a, b):
-        add("g", ("remote", 0), units(src, t, a, b), units(dst, u, a, b),
-            lambda T: (T[dst][:, LANES * u + a:LANES * u + b], T[src][:, LANES * t + a:LANES * t + b]),
-            sem="m%d" % count["msg"], to=to)
+    def send(to, nbytes, r, w, sides):
+        n = count["msg"]
+        add("g", ("remote", nbytes), r, [("left", n)], sides, sem="m%d" % n, to=to)
+        add("", ("lands", nbytes), [("left", n)], w, None, sem="m%d" % n, to=to)
         count["msg"] += 1
-        more(tune["behind"].get((dst, b == LANES), 0), units(dst, u, a, b))
+        pooled(len(ops) - 2)
+        more(tune["behind"], [("left", n)])
+
+    def send_lanes(to, src, dst, t, u, a, b):
+        send(to, 256 * (b - a), units(src, t, a, b), units(dst, u, a, b), lambda T: (lane(T, dst, u, a, b), lane(T, src, t, a, b)))
+
+    def pooled(after):
+        t, a = count["copy"]
+        b = count["stop"]
+        c = max(a, b - tune["pool"], WIDE - tune["pools"][t + 1])
+        if c < b:
+            i = convert(b - c, tabs(t, c, b), tabs(t + 1, c, b), lambda T: (tab(T, t + 1)[:, c:b], tab(T, t)[:, c:b]))
+            if after is not None:
+                ops[i]["deps"].append(after)
+                ops[i]["soft"] = after
+            count["stop"] = c
 
     def more(n, behind):
         t, a = count["copy"]
-        b = min(a + n, WIDE)
+        b = min(a + n, count["stop"] if n == WIDE else min(count["stop"], WIDE - tune["pools"][t + 1]))
         if b > a:
             copy(t, a, b, behind)
             count["copy"] = (t, b)
+
+    def copy(t, a, b, behind=()):
+        dma(512 * (b - a), tabs(t, a, b) + list(behind), tabs(t + 1, a, b),
+            lambda q, T: q.dma_start(tab(T, t + 1)[:, a:b], tab(T, t)[:, a:b]))
+
+    def last_column(t):
+        dma(8192, tabs(t, 0, 1), [("end", t)], lambda q, T: q.dma_start(tab(T, t)[:, WIDE:WIDE + 1], tab(T, t)[:, 0:1]))
 
     def lane(T, name, t, a, b):
         return T[name][:, LANES * t + a:LANES * t + b]
 
     def tabs(t, a=0, b=WIDE):
-        return units("tab", t % NTAB, a, b, 256)
+        return units("tab", t, a, b, 128)
 
     def tab(T, t):
-        return T["tab%d" % (t % NTAB)]
+        return T["tab%d" % t]
 
     def bank():
         count["bank"] += 1
         return "ps%d" % ((count["bank"] - 1) % NBANK)
 
+    def parts(a, b):
+        return [(h, max(a, 128 * h), min(b, 128 * h + 128)) for h in range(a // 128, (b + 127) // 128)]
+
+    def const(q, T, out, n, which, start, stop=False):
+        rows = SUMS[which][1]
+        return q.matmul(out, T.cut[0:rows, 128 * which:128 * which + 128], T.ones[0:rows, 0:n], start, stop)
+
+    def scaled(eng, n, r, w, sides, plus):
+        if eng == "v":
+            add("v", ("el", n), r, w, lambda q, T: q.tensor_scalar(sides(T)[0], sides(T)[1], plus, None, A.add))
+        else:
+            add("s", ("el", n), r, w, lambda q, T: q.activation(sides(T)[0], sides(T)[1], AF.Identity, bias=plus))
+
+    def convert(n, r, w, sides):
+        return add("g", ("gp", n), r, w, lambda q, T: q.affine_select(sides(T)[0], sides(T)[1], [[0, n]], A.is_ge, 0.0, 0, 0))
+
     for n, (a, b) in enumerate(tune["loads"]):
-        dma("y" if n % 2 == 0 else "s", 512 * (b - a), [], units("pm", 0, a, b, 128),
-            lambda q, T, a=a, b=b: q.dma_start(T.pmi[:, a:b], T.pm[:, a:b]), fixed=True)
-        if n == 2:
-            dma("y", 512 * LANES, [], ["si"], lambda q, T: q.dma_start(T.si[:], T.sa[:]), fixed=True)
-    dma("y", 512 * LANES, [], ["ti"], lambda q, T: q.dma_start(T.ti[:], T.ta[:]), fixed=True)
-    add("v", ("el", 1024), [], ["ones"], lambda q, T: q.memset(T.ones[:], 1.0))
+        dma(512 * (b - a), [], units("pm", 0, a, b, 128), lambda q, T, a=a, b=b: q.dma_start(T.pmi[:, a:b], T.pm[:, a:b]))
+        if n == tune["sa"]:
+            dma(512 * LANES, [], ["si"], lambda q, T: q.dma_start(T.si[:], T.sa[:]))
+    add("v", ("el", 128), [], ["ones"], lambda q, T: q.memset(T.ones[:, 0:256], 1.0))
+    add("v", ("el", 896), [], ["many"], lambda q, T: q.memset(T.ones[:, 256:2048], 1.0))
     add("v", ("el", 16), [], ["pad"], lambda q, T: q.memset(T.dm[:, 0:16], 0.0))
-    add("v", ("el", 128), [], ["cut"], lambda q, T: q.memset(T.cut[0:32, 0:LANES], CUT / 32))
-    add("v", ("el", 128), ["cut"], ["cut"], lambda q, T: q.memset(T.cut[32:64, 0:LANES], MID / 32))
-    add("v", ("el", 16), ["cut"], ["cut"], lambda q, T: q.memset(T.cut[0:32, LANES:LANES + 16], CUT16 / 32))
+    for n, (x, rows) in enumerate(SUMS[:5]):
+        add("s", ("el", 128), ["ones"], [("cut", n)],
+            lambda q, T, n=n, x=x / rows: q.activation(T.cut[:, 128 * n:128 * n + 128], T.ones[:, 0:128], AF.Identity, scale=x))
     add("g", ("gp", 16), [], ["x1"], lambda q, T: q.iota(T.x1[:], [[0, 16]], 0, 16))
-    add("g", ("gp", 16), [], ["x2"], lambda q, T: q.iota(T.x2[:], [[256, 16]], 0, 0))
     add("g", ("gp", 256), ["ones"], ["eye"],
         lambda q, T: q.affine_select(T.eye[:], T.ones[:, 0:256], [[0, 2], [-1, 128]], A.is_equal, 0.0, 0, 1))
-    add("g", ("gp", 2048), ["ones"], ["dm"],
+    add("g", ("gp", 16), ["eye"], ["x2"], lambda q, T: q.iota(T.x2[:], [[256, 16]], 0, 0))
+    ops[-1]["soft"] = len(ops) - 2
+    add("g", ("gp", 2048), ["ones", "many"], ["dm"],
         lambda q, T: q.affine_select(T.dm[:, 16:2064], T.ones[:], [[-1, 16], [-512, 8], [-31, 16]], A.is_equal, 0.0, 0, 32))
     add("v", ("el", 16), ["x1"], ["x3"], lambda q, T: q.tensor_scalar(T.x3[:], T.x1[:], 255, None, A.bitwise_and))
     add("v", ("el", 32), ["x3", "x2"], ["x4"], lambda q, T: q.tensor_tensor(T.x4[:], T.x3[:], T.x2[:], A.add))
     add("v", ("el", 16), ["x4"], ["base"], lambda q, T: q.tensor_scalar(T.base[:], T.x4[:], 7.5, None, A.add))
-    add("s", ("el", 128), ["eye"], ["eye32"], lambda q, T: q.activation(T.eye32[:], T.eye[:, 0:128], AF.Copy))
-    add("s", ("el", 255), ["eye"], ["rot"], lambda q, T: q.activation(T.rot[:, 0:255], T.eye[:, 1:256], AF.Copy))
-    add("s", ("el", 16), ["eye"], ["rot"], lambda q, T: q.activation(T.rot[:, 15:256:16], T.eye[:, 0:256:16], AF.Copy))
-    add("v", ("el", LANES), ["si"], units("sl", 0, 0, LANES),
-        lambda q, T: q.tensor_scalar(lane(T, "sl", 0, 0, LANES), T.si[:], -MID, None, A.add))
+    add("s", ("el", 256), ["eye"], ["neg"], lambda q, T: q.activation(T.neg[:], T.eye[:], AF.Identity, scale=-1.0))
+    add("v", ("el", 256), ["eye"], ["rot"], lambda q, T: q.tensor_tensor(T.rot[:, 0:255], T.eye[:, 0:255], T.eye[:, 1:256], A.add))
+    add("v", ("el", 32), ["eye"], ["rot"], lambda q, T: q.tensor_tensor(T.rot[:, 15:256:16], T.eye[:, 15:256:16], T.eye[:, 0:256:16], A.add))
+    convert(128, ["rot", "dm"], ["rot32"], lambda T: (T.eye32[:, 256:384], T.rot[:, 0:128]))
+    scaled("v", LANES, ["si"], units("sl", 0, 0, LANES), lambda T: (lane(T, "sl", 0, 0, LANES), T.si[:]), -MID)
+
+    def late_constants(t):
+        r = ["eye", "neg", ("md", t)]
+        add("g", ("gp", 128), r, [("cut", 5)],
+            lambda q, T: q.affine_select(T.cut[:, 640:768], T.ones[:, 0:128], [[0, 128]], A.is_gt, SUMS[5][0] / SUMS[5][1], 0, 0))
+        convert(128, r, ["eye32"], lambda T: (T.eye32[:, 0:128], T.eye[:, 0:128]))
+        convert(128, r, ["neg32"], lambda T: (T.eye32[:, 128:256], T.neg[:, 0:128]))
 
     def index1(t, a, b, ps):
-        n, o = b - a, 112 if t else 0
-
-        how = tune["mod1"]
-
-        def sums(q, T, extra):
-            q.matmul(T[ps][:, 0:n], T.eye[:, o:o + 128], lane(T, "sl", t, a, b), True, False)
-            if how == "tt":
-                rows = 64 if plain else 32
-                q.matmul(T[ps][:, 0:n], T.ones[0:rows, 0:128], T.cut[0:rows, 0:n], False, False)
-            elif extra is not None:
-                q.matmul(T[ps][:, 0:n], T.eye[:, 0:128], extra, False, False)
-            return q.matmul(T[ps][:, 0:n], T.eye32[:], tab(T, t)[:, 16 * a + t:16 * b:16], False, True)
-        r = ["eye", "eye32"] + units("sl", t, a, b) + tabs(t, 16 * a, 16 * b)
-        if how == "tt":
-            add("p", ("mm", [n, n, max(n, 64) * 4]), r + ["cut", "ones"], [ps], lambda q, T: sums(q, T, None))
+        n, o, turned = b - a, 112 if t else 0, t - 1 in tune["turn_s"]
+        wide = t in tune["wide"]
+        if wide:
+            convert(n, tabs(t, 16 * a, 16 * b), units("pn", t, a, b), lambda T: (lane(T, "pw", t, a, b), tab(T, t)[:, 16 * a + t:16 * b:16]))
         else:
-            add("p", ("mm", [n, max(n, 64) * 4]), r, [ps], lambda q, T: sums(q, T, None))
-        if how == "again":
-            add("s", ("el", n), [], [ps, ("m1", t, a)],
-                lambda q, T: q.activation(lane(T, "m1", t, a, b), T[ps][:, 0:n], AF.Identity, bias=-(CUT - 2047.5), scale=-1.0))
-            add("p", ("mm", [n, n, max(n, 64) * 4]), r + [("m1", t, a)], [ps], lambda q, T: sums(q, T, lane(T, "m1", t, a, b)))
-            add("v", ("el", n), [], [ps] + units("o1", t, a, b),
-                lambda q, T: q.tensor_scalar(lane(T, "o1", t, a, b), T[ps][:, 0:n], CUT, None, A.add))
-        else:
-            remainder(how, ps, "o1", "m1", t, a, b, 2 * MID)
+            scaled("s", n, tabs(t, 16 * a, 16 * b), units("pn", t, a, b),
+                   lambda T: (lane(T, "pn", t, a, b), tab(T, t)[:, 16 * a + t:16 * b:16]), -MID)
 
-    def remainder(how, ps, name, tmp, t, a, b, plus):
-        n = b - a
-        if how == "tt":
-            if tune[tmp] == "s":
-                add("s", ("el", n), [], [ps, (tmp, t, a)],
-                    lambda q, T: q.activation(lane(T, tmp, t, a, b), T[ps][:, 0:n], AF.Identity, bias=2047.5, scale=-1.0))
-            else:
-                add("v", ("el", n), [], [ps, (tmp, t, a)],
-                    lambda q, T: q.tensor_scalar(lane(T, tmp, t, a, b), T[ps][:, 0:n], -1.0, 2047.5, A.mult, A.add))
-            add("v", ("el", n), [(tmp, t, a)], [ps] + units(name, t, a, b),
-                lambda q, T: q.tensor_tensor(lane(T, name, t, a, b), T[ps][:, 0:n], lane(T, tmp, t, a, b), A.add))
-        else:
-            w = 256 * (count["int"] % 2)
-            count["int"] += 1
-            add("v", ("el", n), [], [ps, ("w1", w)], lambda q, T: q.tensor_scalar(T.w1[:, w:w + n], T[ps][:, 0:n], plus, None, A.add))
-            add("v", ("el", n), [("w1", w)], [("w2", w)],
-                lambda q, T: q.tensor_scalar(T.w2[:, w:w + n], T.w1[:, w:w + n], WIDE - 1, None, A.bitwise_and))
-            add("v", ("el", n), [("w2", w)], units(name, t, a, b), lambda q, T: q.tensor_copy(lane(T, name, t, a, b), T.w2[:, w:w + n]))
+        def sums(q, T):
+            def both(eye, eye32, stop):
+                if turned:
+                    for h, c, d in parts(a, b):
+                        w = SW * (2 * t + h)
+                        q.matmul(T[ps][:, c - a:d - a], T.sv[:, w:w + 128], eye[:, c - 128 * h:d - 128 * h], False, False)
+                else:
+                    q.matmul(T[ps][:, 0:n], eye[:, o:o + 128], lane(T, "sl", t, a, b), False, False)
+                if wide:
+                    return q.matmul(T[ps][:, 0:n], eye32, lane(T, "pw", t, a, b), False, stop)
+                return q.matmul(T[ps][:, 0:n], eye[:, 0:128], lane(T, "pn", t, a, b), False, stop)
+            const(q, T, T[ps][:, 0:n], n, 5 if wide else 0, True)
+            both(T.neg, T.eye32[:, 128:256], False)
+            const(q, T, T[ps][:, 0:n], n, 1, False)
+            const(q, T, T[ps][:, 0:n], n, 2, False)
+            return both(T.eye, T.eye32[:, 0:128], True)
+        r = [("sv", t, h) for h, _, _ in parts(a, b)] if turned else units("sl", t, a, b)
+        r += ["eye", "neg", "ones", ("cut", 0), ("cut", 1), ("cut", 2)] + (["eye32", "neg32", ("cut", 5)] if wide else [])
+        add("p", ("mm", [n] * (13 if wide else 7)), r + units("pn", t, a, b), [ps], sums)
+        scaled("s" if "o1" in tune["on_s"] and t else "v", n, [], [ps] + units("o1", t, a, b),
+               lambda T: (lane(T, "o1", t, a, b), T[ps][:, 0:n]), MID if wide else 0.0)
 
-    def last_column(t):
-        dma("y", 8192, tabs(t, 0, 1), [("end", t % NTAB)], lambda q, T: q.dma_start(tab(T, t)[:, WIDE:WIDE + 1], tab(T, t)[:, 0:1]))
-
-    def copy(t, a, b, behind):
-        dma("y", 512 * (b - a), tabs(t, a, b) + behind, tabs(t + 1, a, b),
-            lambda q, T: q.dma_start(tab(T, t + 1)[:, a:b], tab(T, t)[:, a:b]))
-
-    for a, b in tune["pieces"]:
-        n, ps = b - a, bank()
-        pmr = units("pm", 0, a, b, 128)
-        if plain:
-            add("v", ("el", n), pmr, tabs(0, a, b),
-                lambda q, T, a=a, b=b: q.tensor_scalar(T.tab0[:, a:b], T.pmi[:, a:b], WIDE - 1, None, A.bitwise_and))
-            if a in tune["plain"]:
-                add("v", ("el", n), pmr, tabs(0, HALF + a, HALF + b),
-                    lambda q, T, a=a, b=b: q.tensor_scalar(T.tab0[:, HALF + a:HALF + b], T.pmi[:, a:b], 12, None, A.logical_shift_right))
-            else:
-                add("s", ("el", n), pmr, [("hh", a)],
-                    lambda q, T, a=a, b=b: q.activation(T.hi[:, a:b], T.pmi[:, a:b], AF.Identity,
-                                                        bias=-(2047.0 + 2047.5 / WIDE), scale=1.0 / WIDE))
-                add("s", ("el", n), [("hh", a)], tabs(0, HALF + a, HALF + b),
-                    lambda q, T, a=a, b=b: q.activation(T.tab0[:, HALF + a:HALF + b], T.hi[:, a:b], AF.Identity, bias=2047.0))
-        else:
-            add("v", ("el", n), pmr, [("hh", a)],
-                lambda q, T, a=a, b=b: q.tensor_scalar(T.hh[:, a:b], T.pmi[:, a:b], -8386559.5, BIG, A.add, A.add))
-            add("s", ("el", n), [("hh", a)], tabs(0, HALF + a, HALF + b),
-                lambda q, T, a=a, b=b: q.activation(T.tab0[:, HALF + a:HALF + b], T.hh[:, a:b], AF.Identity,
-                                                    bias=-(BIG / WIDE + 1.0), scale=1.0 / WIDE))
-            add("s", ("el", n), tabs(0, HALF + a, HALF + b), [ps],
-                lambda q, T, a=a, b=b, ps=ps: q.activation(T[ps][:, 0:b - a], T.tab0[:, HALF + a:HALF + b], AF.Identity,
-                                                           bias=WIDE * MID + MID, scale=float(WIDE)))
-            add("v", ("el", n), pmr, [ps] + tabs(0, a, b),
-                lambda q, T, a=a, b=b, ps=ps: q.tensor_tensor(T.tab0[:, a:b], T.pmi[:, a:b], T[ps][:, 0:b - a], A.subtract))
+    for a, b, v in tune["pieces"]:
+        pmr, c = units("pm", 0, a, b, 128), a + v
+        if c < b:
+            add("s", ("el", b - c), pmr, [("hi", a)],
+                lambda q, T, c=c, b=b: q.activation(T.hi[:, c:b], T.pmi[:, c:b], AF.Identity,
+                                                    bias=-(2047.0 + 2047.5 / WIDE), scale=1.0 / WIDE))
+            add("s", ("el", b - c), [("hi", a)], tabs(0, HALF + c, HALF + b),
+                lambda q, T, c=c, b=b: q.activation(T.tab0[:, HALF + c:HALF + b], T.hi[:, c:b], AF.Identity, bias=2047.0))
+        add("v", ("el", b - a), pmr, tabs(0, a, b),
+            lambda q, T, a=a, b=b: q.tensor_scalar(T.tab0[:, a:b], T.pmi[:, a:b], WIDE - 1, None, A.bitwise_and))
+        if v:
+            add("v", ("el", v), pmr, tabs(0, HALF + a, HALF + c),
+                lambda q, T, a=a, c=c: q.tensor_scalar(T.tab0[:, HALF + a:HALF + c], T.pmi[:, a:c], 12, None, A.logical_shift_right))
+        for c, d in tune["seq"][0][2]:
+            if a < max(16 * (y - 128 * h) for h, _, y in parts(c, d)) <= b:
+                index1(0, c, d, bank())
         if b in (1024, 2048):
-            index1(0, b // 16 + 64, b // 16 + 128, "ps6")
-            index1(0, b // 16 - 64, b // 16, "ps7")
-            copy(0, HALF + b - 1024, HALF + b, [])
-            copy(0, b - 1024, b, [])
+            for x in (0, HALF):
+                c = x + b - 1024 + (max(0, min(1024, tune["pools"][1] - x // 2)) if b == 1024 else 0)
+                if c > x + b - 1024:
+                    convert(c - x, ["dm"] + tabs(0, x, c), tabs(1, x, c), lambda T, x=x, c=c: (T.tab1[:, x:c], T.tab0[:, x:c]))
+                if c < x + b:
+                    copy(0, c, x + b)
     last_column(0)
 
-    done = {}
-
-    def gather(k, t, a, b, c):
-        last = t == STEPS - 1
-        n = b - a
-        if k == 1:
-            r0 = RING + a
-        else:
-            if count["ring"] + n > RING:
-                count["ring"] = 0
-            r0 = count["ring"]
-            count["ring"] += n
-        s0 = 16 * r0
+    def gather(k, t, a, b, tile, whole):
+        last, n = t == STEPS - 1, b - a
+        s0 = WIDE * tile
         off, wide = "o%d" % k, WIDE + 1 if k == 4 else WIDE
-        tr = tabs(t) + ([("end", t % NTAB)] if k == 4 else [])
+        r = tabs(t) + ([("end", t)] if k == 4 else []) + units(off, t, a, b)
+        got = units("gv", tile, a, b) + units("gs", tile, a, b)
+        cut = [a]
 
         def by_vector(q, T):
-            out, win = T.gg[:, s0:s0 + 16 * (c - a)], tab(T, t)[:, 0:wide].indirect(lane(T, off, t, a, c))
-            return q.tensor_scalar(out, win, -MID, None, A.add) if plain else q.tensor_copy(out, win)
+            c = cut[0]
+            return q.tensor_scalar(T.gg[:, s0 + 16 * a:s0 + 16 * c], tab(T, t)[:, 0:wide].indirect(lane(T, off, t, a, c)), -MID, None, A.add)
 
         def by_scalar(q, T):
-            out, win = T.gg[:, s0 + 16 * (c - a):s0 + 16 * n], tab(T, t)[:, 0:wide].indirect(lane(T, off, t, c, b))
-            return q.activation(out, win, AF.Identity, bias=-MID) if plain else q.activation(out, win, AF.Copy)
-        add("v", ("gather", 16 * (c - a)), tr + units(off, t, a, c), units("gg", 0, r0, r0 + c - a, 2), by_vector, fixed=True)
-        add("s", ("gather", 16 * (b - c)), tr + units(off, t, c, b), units("gg", 0, r0 + c - a, r0 + n, 2), by_scalar, fixed=True)
-        ps, o = bank(), 112 if t else 0
-        turned = k in tune["turn"] and n <= 128
-        if turned:
-            p0, y0 = bank(), 128 * (count["turn"] % 4)
-            count["turn"] += 1
+            c = cut[0]
+            return q.activation(T.gg[:, s0 + 16 * c:s0 + 16 * b], tab(T, t)[:, 0:wide].indirect(lane(T, off, t, c, b)), AF.Identity, bias=-MID)
+        x = add("v", ("gather", 8 * n), r, [], by_vector, fixed=True)
+        y = add("s", ("gather", 8 * n), r, [], by_scalar, fixed=True)
+        for z in (x, y):
+            ops[z]["deps"] = sorted(set(ops[z]["deps"]).union(*[read.get(u, ()) for u in got]))
+        for u in got:
+            wrote[u], read[u] = x if u[0] == "gv" else y, []
+        pairs.append((x, y, a, b, cut))
+        ps = bank()
+
+        def offsets(name, plus, ps=ps):
+            scaled("s" if name in tune["on_s"] else "v", n, [], [ps] + units(name, t, a, b),
+                   lambda T: (lane(T, name, t, a, b), T[ps][:, 0:n]), plus)
+
+        def keep(name):
+            scaled("s", n, [], [ps] + units(name, t, a, b), lambda T: (lane(T, name, t, a, b), T[ps][:, 0:n]), 0.0)
+
+        if k == 1 and t in tune["turn_s"]:
+            halves = [h for h, _, _ in parts(a, b)]
+            h0, h1 = halves[0], halves[-1] + 1
 
             def turn(q, T):
-                for j in range(16):
-                    m = q.matmul(T[p0][0:n, j:128:16], T.gg[:, s0 + j:s0 + 16 * n:16], T.eye[:, j:128:16], True, True)
+                for h in halves:
+                    for j in range(16):
+                        w = SW * (h - h0)
+                        m = q.matmul(T[ps][:, w + j:w + SW:16], T.gg[:, s0 + HALF * h + j:s0 + HALF * (h + 1):16],
+                                     T.eye[:, 112 + j:256:16], True, True)
                 return m
-            add("p", ("mm", [8] * 16), ["eye"] + units("gg", 0, r0, r0 + n, 2), [p0], turn)
-            if tune["turn"][k] == "s":
-                add("s", ("el", 128), [], [p0, ("yy", y0)], lambda q, T: q.activation(T.yy[0:n, y0:y0 + 128], T[p0][0:n, 0:128], AF.Copy))
-            else:
-                add("v", ("el", 128), [], [p0, ("yy", y0)], lambda q, T: q.tensor_copy(T.yy[0:n, y0:y0 + 128], T[p0][0:n, 0:128]))
+            add("p", ("mm", [64] * 16 * len(halves)), ["eye"] + got, [ps], turn)
+            w0, w1, mine = SW * (2 * t + h0), SW * (2 * t + h1), [("su", t, h) for h in halves]
+            scaled("s", w1 - w0, [], [ps] + mine, lambda T: (T.su[:, w0:w1], T[ps][:, 0:w1 - w0]), 0.0)
+            send(1, 256 * (w1 - w0), mine, [("sv", t + 1, h) for h in halves],
+                 lambda T: (T.sv[:, w0 + 2 * SW:w1 + 2 * SW], T.su[:, w0:w1]))
+            back = bank()
 
-        def pick(q, T):
-            if turned:
-                m = q.matmul(T[ps][:, 0:n], T.yy[0:n, y0:y0 + 128], T.eye[0:n, 0:n], True, k != 4)
-            else:
-                for j in range(16):
-                    m = q.matmul(T[ps][:, 0:n], T.dm[:, 16 + 128 * j:144 + 128 * j], T.gg[:, s0 + j:s0 + 16 * n:16],
-                                 j == 0, j == 15 and k != 4)
-            if k == 4:
-                if tune["mod5"] == "tt":
-                    q.matmul(T[ps][:, 0:n], T.ones[0:64, 0:128], T.cut[0:64, 0:n], False, False)
-                q.matmul(T[ps][:, 0:n], T.eye[:, o:o + 128], lane(T, "tl", t, a, b), False, False)
-                m = q.matmul(T[ps][:, 0:n], T.rot[:, o:o + 128], lane(T, "tl", t, a, b), False, True)
-            return m
-        r = ["eye", ("yy", y0)] if turned else ["dm"] + units("gg", 0, r0, r0 + n, 2)
-        r += ["eye", "rot", "cut", "ones"] + units("tl", t, a, b) if k == 4 else []
-        add("p", ("mm", [n] * ((1 if turned else 16) + ((3 if tune["mod5"] == "tt" else 2) if k == 4 else 0))), r, [ps], pick)
-
-        def offsets(name, plus):
-            add("v", ("el", n), [], [ps] + units(name, t, a, b),
-                lambda q, T: q.tensor_scalar(lane(T, name, t, a, b), T[ps][:, 0:n], plus, None, A.add))
-
-        def keep(name, col):
-            if last:
-                add("s", ("el", n), [], [ps] + units(name, t, a, b),
-                    lambda q, T: q.activation(T.yo[:, col + a:col + b], T[ps][:, 0:n], AF.Identity, bias=MID))
-            else:
-                add("s", ("el", n), [], [ps] + units(name, t, a, b),
-                    lambda q, T: q.activation(lane(T, name, t, a, b), T[ps][:, 0:n], AF.Copy))
-        done[(k, t)] = done.get((k, t), 0) + n
-        whole = done[(k, t)] == LANES
-        if k == 1:
-            offsets("o2", MID)
-            keep("s16", 0)
-            if whole and last:
-                dma("y", 512 * LANES, units("s16", t, 0, LANES), [], lambda q, T: q.dma_start(T.ys[:], T.yo[:, 0:LANES]))
-            elif t == 0 and a == 0:
-                send(1, "s16", "sl", t, t + 1, a, b)
-                done["early"] = b
-            if whole and not last:
-                send(1, "s16", "sl", t, t + 1, done.pop("early", 0), LANES)
-                places(t)
-        elif k == 2:
-            offsets("z1s", MID)
-            send(1, "z1s", "o3", t, t, a, b)
-        elif k == 3:
-            offsets("z2s", MID + 1.0)
-            send(-1, "z2s", "o4", t, t, a, b)
-        elif k == 4:
-            remainder(tune["mod5"], ps, "o5", "m5", t, a, b, 3 * MID)
+            def turn_back(q, T):
+                for h in halves:
+                    w = SW * (2 * t + h) + 16
+                    m = q.matmul(T[back][:, 128 * (h - h0):128 * (h - h0 + 1)], T.su[:, w:w + 128], T.eye[:, 0:128], True, True)
+                return m
+            add("p", ("mm", [128] * len(halves)), ["eye"] + mine, [back], turn_back)
+            offsets("o2", MID, back)
         else:
-            keep("t16", LANES)
-            if last:
-                dma("y", 512 * n, units("t16", t, a, b), [],
-                    lambda q, T: q.dma_start(T.yt[:, a:b], T.yo[:, LANES + a:LANES + b]))
-            elif t == STEPS - 2:
-                send(1, "t16", "tl", t, t + 1, a, b)
-            elif whole:
-                send(1, "t16", "tl", t, t + 1, 0, LANES)
+            def pick(q, T):
+                for j in range(16):
+                    m = q.matmul(T[ps][:, 0:n], T.dm[:, 16 + 128 * j:144 + 128 * j], T.gg[:, s0 + 16 * a + j:s0 + 16 * b:16],
+                                 j == 0, j == 15 and k != 4)
+                return m
+            add("p", ("mm", [n] * 16), ["dm"] + got, [ps], pick)
+            if k == 1:
+                offsets("o2", MID)
+                if not last:
+                    keep("s16")
+                    send_lanes(1, "s16", "sl", t, t + 1, a, b)
+                else:
+                    convert(n, units("o2", t, a, b), units("s16", t, a, b), lambda T: (T.yo[:, a:b], lane(T, "o2", t, a, b)))
+                    if whole:
+                        dma(512 * LANES, units("s16", t, 0, LANES), [], lambda q, T: q.dma_start(T.ys[:], T.yo[:, 0:LANES]))
+            elif k == 2:
+                offsets("z1s", MID)
+                send_lanes(1, "z1s", "o3", t, t, a, b)
+            elif k == 3:
+                offsets("z2s", MID + 1.0)
+                send_lanes(-1, "z2s", "o4", t, t, a, b)
+            elif k == 4:
+                index5(t, a, b, ps)
+            elif not last:
+                keep("t16")
+                send_lanes(1, "t16", "tl", t, t + 1, a, b)
+            else:
+                scaled("s", n, [], [ps] + units("t16", t, a, b), lambda T: (T.yo[:, LANES + a:LANES + b], T[ps][:, 0:n]), MID)
+                dma(512 * n, units("t16", t, a, b), [], lambda q, T: q.dma_start(T.yt[:, a:b], T.yo[:, LANES + a:LANES + b]))
+        if k == 1 and whole and not last:
+            places(t, s0, tile)
 
-    def places(t):
+    def index5(t, a, b, ps):
+        n = b - a
+
+        def sums(q, T):
+            if t:
+                q.matmul(T[ps][:, 0:n], T.rot[:, 112:240], lane(T, "tl", t, a, b), False, False)
+            else:
+                q.matmul(T[ps][:, 0:n], T.eye32[:, 256:384], T.tw[:, a:b], False, False)
+            return const(q, T, T[ps][:, 0:n], n, 3, False, True)
+        add("p", ("mm", [max(n, 64) * (2 if t else 5)]), units("tl", t, a, b) + ["rot", "rot32", ("cut", 3)], [ps], sums)
+        add("s", ("el", n), [], [ps, ("m5", t, a)],
+            lambda q, T: q.activation(lane(T, "m5", t, a, b), T[ps][:, 0:n], AF.Identity, bias=2047.5, scale=-1.0))
+        add("v", ("el", n), [("m5", t, a)], [ps] + units("o5", t, a, b),
+            lambda q, T: q.tensor_tensor(lane(T, "o5", t, a, b), T[ps][:, 0:n], lane(T, "m5", t, a, b), A.add))
+
+    def places(t, s0, tile):
         def spread(q, T):
             for j in range(16):
-                q.matmul(T.ps7[:, 0:16], T.dm[:, 16 - j:144 - j], T.gg[:, 16 * (RING + j):16 * (RING + LANES):256], j == 0, False)
-            return q.matmul(T.ps7[:, 0:16], T.ones[0:32, 0:128], T.cut[0:32, LANES:LANES + 16], False, True)
-        add("p", ("mm", [16] * 17), ["dm", "pad", "ones", "cut"] + units("gg", 0, RING, RING + LANES, 2), ["ps7"], spread)
-        add("v", ("el", 16), ["base"], ["ps7", ("md", t)],
-            lambda q, T: q.tensor_tensor(T.md[:, 16 * t:16 * t + 16], T.base[:], T.ps7[:, 0:16], A.subtract))
-        if tune["md"] == "tt":
-            add("v", ("el", 16), [("md", t)], ["ps7", ("li", t)],
-                lambda q, T: q.tensor_tensor(T.li[:, 16 * t:16 * t + 16], T.ps7[:, 0:16], T.md[:, 16 * t:16 * t + 16], A.add))
-        else:
-            add("v", ("el", 16), [("md", t)], ["ps7", "d1"],
-                lambda q, T: q.tensor_tensor(T.d1[:], T.ps7[:, 0:16], T.md[:, 16 * t:16 * t + 16], A.add))
-            add("v", ("el", 16), ["d1"], [("li", t)], lambda q, T: q.tensor_copy(T.li[:, 16 * t:16 * t + 16], T.d1[:]))
+                q.matmul(T.ps6[:, 0:16], T.dm[:, 16 - j:144 - j], T.gg[:, s0 + 16 * j:s0 + WIDE:256], j == 0, False)
+            return const(q, T, T.ps6[:, 0:16], 16, 4, False, True)
+        add("p", ("mm", [16] * 17), ["dm", "pad", ("cut", 4)] + units("gv", tile, 0, LANES) + units("gs", tile, 0, LANES), ["ps6"], spread)
+        add("v", ("el", 16), ["base"], ["ps6", ("md", t)],
+            lambda q, T: q.tensor_tensor(T.md[:, 16 * t:16 * t + 16], T.base[:], T.ps6[:, 0:16], A.subtract))
+        add("v", ("el", 16), [("md", t)], ["ps6", ("li", t)],
+            lambda q, T: q.tensor_tensor(T.li[:, 16 * t:16 * t + 16], T.ps6[:, 0:16], T.md[:, 16 * t:16 * t + 16], A.add))
 
-    def swap(t):
+    def swap(t, chunks):
         more(WIDE, [])
-        if tune["bg"] == "s":
-            add("s", ("gather", LANES), tabs(t) + [("li", t)], tabs(t + 1),
-                lambda q, T: q.activation(tab(T, t + 1)[:, t:WIDE:16], tab(T, t)[:, 0:WIDE].indirect(T.li[:, 16 * t:16 * t + 16]), AF.Copy))
-        else:
-            add("v", ("gather", LANES), tabs(t) + [("li", t)], tabs(t + 1),
-                lambda q, T: q.tensor_copy(tab(T, t + 1)[:, t:WIDE:16], tab(T, t)[:, 0:WIDE].indirect(T.li[:, 16 * t:16 * t + 16])))
+        if t + 1 == min(tune["wide"]):
+            late_constants(t)
         add("v", ("scatter", LANES), tabs(t) + [("li", t)], tabs(t + 1),
             lambda q, T: q.tensor_copy(tab(T, t + 1)[:, 0:WIDE].indirect(T.li[:, 16 * t:16 * t + 16]), tab(T, t)[:, t:WIDE:16]))
+        add("s", ("gather", LANES), tabs(t) + [("li", t)], tabs(t + 1),
+            lambda q, T: q.activation(tab(T, t + 1)[:, t:WIDE:16], tab(T, t)[:, 0:WIDE].indirect(T.li[:, 16 * t:16 * t + 16]), AF.Copy))
+        for a, b in chunks:
+            index1(t + 1, a, b, "ps6")
         if t == 0:
-            add("v", ("el", LANES), ["ti", ("li", 0)], units("tl", 0, 0, LANES),
-                lambda q, T: q.tensor_scalar(lane(T, "tl", 0, 0, LANES), T.ti[:], -MID, None, A.add))
+            dma(512 * LANES, [("left", 0)], ["ti"], lambda q, T: q.dma_start(T.ti[:], T.ta[:]))
+            convert(LANES, ["ti"], units("tl", 0, 0, LANES), lambda T: (T.tw[:], T.ti[:]))
         last_column(t + 1)
-        index1(t + 1, 0, LANES, "ps6")
         if t < STEPS - 2:
-            for a in range(0, tune["gcopy"], 512):
-                add("g", ("gp", 512), tabs(t + 1, a, a + 512), tabs(t + 2, a, a + 512),
-                    lambda q, T, a=a: q.affine_select(tab(T, t + 2)[:, a:a + 512], tab(T, t + 1)[:, a:a + 512], [[0, 512]],
-                                                      A.is_ge, 0.0, 0, 0))
-            count["copy"] = (t + 1, tune["gcopy"])
-            more(tune["behind"].get("now", 0), [])
+            count["copy"], count["stop"] = (t + 1, 0), WIDE
+            pooled(None)
+            more(tune["now"][t], [])
 
-    for k, t, a, b, v in tune["seq"]:
-        if k:
-            gather(k, t, a, b, a + v)
-        else:
-            swap(t)
-    return ops
+    for k, t, chunks in tune["seq"]:
+        if k == 0:
+            swap(t, [c for j, u, c in tune["seq"] if (j, u) == (1, t + 1)][0])
+            continue
+        tile = count["tile"] % NG
+        count["tile"] += 1
+        for a, b in chunks:
+            gather(k, t, a, b, tile, (a, b) == chunks[-1])
+    return ops, pairs
 
 
 def spans(op, M, state, start):
     kind, n = op["cost"]
     if kind == "dma":
-        at = max(start + M["dma"] / 2, state.get("dma", 0.0)) + n / M["bw"]
-        state["dma"] = at
-        return start + M["dhold"], at + M["dma"] / 2
+        state["dma"] = max(start + M["dma"] / 2, state.get("dma", 0.0)) + n / M["bw"]
+        return start + M["dhold"], state["dma"] + M["dma"] / 2
     if kind == "remote":
         extra = 0.0 if state.get("sent") else M["first"]
         state["sent"] = True
-        at = max(start + extra + M["remote"] / 3, state.get("dma", 0.0)) + M["remote"] / 3
-        state["dma"] = at
-        return start + M["ghold"] + extra, at + M["remote"] / 3
+        state["dma"] = max(start + extra + M["remote"] / 2, state.get("dma", 0.0)) + n / M["link"]
+        return start + M["ghold"] + extra, state["dma"]
+    if kind == "lands":
+        return 0.0, start + M["remote"] / 2
     if kind == "mm":
         d = sum(max(64, x) * M["pe"] + M["peo"] for x in n)
     elif kind == "gp":
         d = 170.0 + 2 * n * M["cyc"]
     else:
         rate = 1.0 if kind == "el" else M[kind]
-        d = (50.0 if op["eng"] == "v" else 65.0) + max(64, n * rate) * M["cyc"]
+        d = (55.0 if op["eng"] == "v" else 70.0) + max(64, n * rate) * M["cyc"]
     return start + d, start + d
 
 
-def order_ops(ops, tune, M):
+def order_ops(ops, pairs, tune, M, skew):
     n = len(ops)
     left = [len(o["deps"]) for o in ops]
     after = [[] for _ in ops]
     for i, o in enumerate(ops):
         for d in o["deps"]:
             after[d].append(i)
-    chain = {e: [i for i in range(n) if ops[i]["eng"] == e and ops[i]["fixed"]] for e in "vspgy"}
-    head = {e: 0 for e in chain}
-    free = {e: 0.0 for e in chain}
-    end, state, order = [0.0] * n, {}, []
-    due = {i: 0.0 for i in range(n) if not left[i]}
-    while due:
-        best = None
-        for i, r in due.items():
-            o = ops[i]
-            e = o["eng"]
-            if o["fixed"] and chain[e][head[e]] != i:
-                continue
-            s = max(free[e], r)
-            key = (s + (tune["ahead"] if o["fixed"] and o["cost"][0] == "gather" else 0.0), i)
-            if best is None or key < best[0]:
-                best = (key, i, s)
-        _, i, s = best
+    need = [len(pairs)] * n
+    for m, p in enumerate(pairs):
+        need[p[0]] = need[p[1]] = m
+    for i in reversed(range(n)):
+        for d in ops[i]["deps"]:
+            if not ops[d]["fixed"]:
+                need[d] = min(need[d], need[i])
+    for i in range(len(tune["loads"]) + 1):
+        need[i] = -1
+    free = {e: 0.0 for e in ["v", "s", "p", "g", "y", ""]}
+    end, state, order, idle = [0.0] * n, {}, [], []
+    due, ready = {i: 0.0 for i in range(n) if not left[i]}, [0.0] * n
+    column, head, busy = 16 * M["gather"] * M["cyc"], 0, {"v": 0.0, "s": 0.0}
+
+    def slack(o, d):
+        return tune["margin"] if o["eng"] in "vs" and ops[d]["eng"] not in "vs" else 0.0
+
+    def run(i):
         e = ops[i]["eng"]
-        free[e], end[i] = spans(ops[i], M, state, s)
-        if ops[i]["fixed"]:
-            head[e] += 1
+        free[e], end[i] = spans(ops[i], M, state, max(free[e], ready[i]))
         order.append(i)
         del due[i]
         for j in after[i]:
             left[j] -= 1
             if not left[j]:
-                o = ops[j]
-                loose = not o["fixed"] and o["eng"] in "vs"
-                due[j] = max(end[d] + M["sem"] + (tune["margin"] if loose and ops[d]["eng"] != o["eng"] else 0.0) for d in o["deps"])
-    return order
+                hard = [d for d in ops[j]["deps"] if d != ops[j].get("soft")]
+                ready[j] = max([end[d] + M["sem"] for d in hard], default=0.0)
+                due[j] = max([end[d] + M["sem"] + slack(ops[j], d) for d in hard], default=0.0)
+    while due:
+        best = min(((max(free[ops[i]["eng"]], r), need[i], i) for i, r in due.items() if not ops[i]["fixed"]), default=None)
+        if head < len(pairs):
+            x, y, a, b, cut = pairs[head]
+            if x in due and y in due:
+                sv, ss = max(free["v"], ready[x]), max(free["s"], ready[y])
+                if best is None or max(sv, ss) + tune["ahead"] < best[0]:
+                    idle.append(ss - busy["s"] - sv + busy["v"])
+                    v = 2 * round(((b - a) / 2 + (ss - sv - skew[head]) / (2 * column)) / 2)
+                    cut[0] = a + min(max(v, 2), b - a - 2)
+                    ops[x]["cost"], ops[y]["cost"] = ("gather", 16 * (cut[0] - a)), ("gather", 16 * (b - cut[0]))
+                    run(x)
+                    run(y)
+                    busy["v"], busy["s"] = free["v"], free["s"]
+                    head += 1
+                    continue
+        o = ops[best[2]]
+        if o["eng"] in busy:
+            busy[o["eng"]] += spans(o, M, {}, 0.0)[0]
+        run(best[2])
+    return order, idle[1:] + [0.0]
 
 
 PLAN = {}
@@ -453,8 +480,12 @@ PLAN = {}
 
 def plan():
     if not PLAN:
-        ops = make_ops(TUNE)
-        PLAN["ops"], PLAN["order"] = ops, order_ops(ops, TUNE, NOMINAL)
+        ops, pairs = make_ops(TUNE)
+        skew = [0.0] * len(pairs)
+        for _ in range(TUNE["rounds"] + 1):
+            order, idle = order_ops(ops, pairs, TUNE, NOMINAL, skew)
+            skew = [x + TUNE["damp"] * (y + TUNE["skew"]) for x, y in zip(skew, idle)]
+        PLAN["ops"], PLAN["order"] = ops, order
     return PLAN["ops"], PLAN["order"]
 
 
@@ -463,20 +494,20 @@ def rank_program(g, core, T, topo):
     if rank is None:
         return
     ops, order = plan()
+    cores = list(T.cores)
     queue = {"v": g.vector, "s": g.scalar, "p": g.tensor, "g": g, "y": g.sync}
-    peer = {}
-    for to in (1, -1):
-        other = T.cores[(rank + to) % len(T.cores)]
-        rid, pid, _ = topo.addr(other)
-        peer[to] = (pid, rid, topo.mask(core, other), len(topo.engines(core, other)),
-                    len(topo.engines(T.cores[(rank - to) % len(T.cores)], core)))
     mark, know, total = {}, {e: {} for e in queue}, {}
     for i in order:
         o = ops[i]
+        if not o["eng"]:
+            mark[i] = (o["sem"], len(topo.engines(cores[(rank - o["to"]) % len(cores)], core)), {})
+            continue
         e, q = o["eng"], queue[o["eng"]]
         need = {}
         for d in o["deps"]:
             s, val, _ = mark[d]
+            if (e == "p" and s == "p") or d == o.get("soft"):
+                continue
             if need.get(s, (0, None))[0] < val:
                 need[s] = (val, d)
         for s, (val, d) in sorted(need.items(), key=lambda x: -x[1][1]):
@@ -486,11 +517,12 @@ def rank_program(g, core, T, topo):
                 for s2, v2 in mark[d][2].items():
                     know[e][s2] = max(know[e].get(s2, 0), v2)
         if o["to"]:
-            pid, rid, mask, sent, comes = peer[o["to"]]
+            other = cores[(rank + o["to"]) % len(cores)]
+            rid, pid, _ = topo.addr(other)
             out, src = o["emit"](T)
-            g.remote_dma(out, src, T.sem[o["sem"]], T.sem.loc, pid, rid, mask)
-            total["loc"] = total.get("loc", 0) + sent
-            mark[i] = (o["sem"], comes, {})
+            g.remote_dma(out, src, T.sem[o["sem"]], T.sem["l" + o["sem"]], pid, rid, topo.mask(core, other))
+            total["l" + o["sem"]] = len(topo.engines(core, other))
+            mark[i] = ("l" + o["sem"], total["l" + o["sem"]], {})
         elif o["sem"]:
             o["emit"](q, T).then_inc(T.sem[o["sem"]], 16)
             total[o["sem"]] = 16

from concourse.mybir import AluOpType, ActivationFunctionType

STEPS, LANES, WIDE, HALF = 6, 256, 4096, 2048
NG = 5
NBANK = 6
MID = 2048.0
BIG = 51539607552.0
CUT = 786432.0
CUT16 = 24576.0
SUMS = [(MID - 0.5, 65), (BIG, 32), (-BIG, 32), (CUT + MID, 40), (CUT16, 32), (-0.5, 32)]
SW = 144

SCRATCH = {
    "pmi": ("sbuf", [128, HALF], "int32"),
    "si": ("sbuf", [128, LANES], "int32"),
    "ti": ("sbuf", [128, LANES], "int32"),
    "hi": ("sbuf", [128, HALF], "int32"),
    "gg": ("sbuf", [128, WIDE * NG], "float16"),
    "ones": ("sbuf", [128, 2048], "bfloat16"),
    "dm": ("sbuf", [128, 16 + 2048], "bfloat16"),
    "eye": ("sbuf", [128, 256], "bfloat16"),
    "neg": ("sbuf", [128, 256], "bfloat16"),
    "rot": ("sbuf", [128, 256], "bfloat16"),
    "eye32": ("sbuf", [128, 384], "float32"),
    "cut": ("sbuf", [128, 128 * len(SUMS)], "bfloat16"),
    "pw": ("sbuf", [128, LANES * STEPS], "float32"),
    "tw": ("sbuf", [128, LANES], "float32"),
    "x1": ("sbuf", [128, 16], "int32"),
    "x2": ("sbuf", [128, 16], "int32"),
    "x3": ("sbuf", [128, 16], "int32"),
    "x4": ("sbuf", [128, 16], "int32"),
    "base": ("sbuf", [128, 16], "float32"),
    "md": ("sbuf", [128, 16 * STEPS], "float16"),
    "li": ("sbuf", [128, 16 * STEPS], "uint16"),
    "yo": ("sbuf", [128, 2 * LANES], "float32"),
    "m5": ("sbuf", [128, LANES * STEPS], "bfloat16"),
}
for _n in range(STEPS):
    SCRATCH["tab%d" % _n] = ("sbuf", [128, WIDE + 8], "int32")
for _n in ("o1", "o2", "z1s", "o3", "z2s", "o4", "o5"):
    SCRATCH[_n] = ("sbuf", [128, LANES * STEPS], "uint16")
for _n in ("s16", "sl", "t16", "tl", "pn"):
    SCRATCH[_n] = ("sbuf", [128, LANES * STEPS], "float16")
for _n in ("su", "sv"):
    SCRATCH[_n] = ("sbuf", [128, 2 * SW * STEPS], "float16")
for _n in range(NBANK + 1):
    SCRATCH["ps%d" % _n] = ("psum", [128, 512], "float32")
NMSG, NDMA = 50, 46
SEMAPHORES = ["v", "s", "p", "g"] + [_x % _n for _x in ("m%d", "lm%d") for _n in range(NMSG)] + ["d%d" % _n for _n in range(NDMA)]

NOMINAL = dict(cyc=0.96, gather=1.45, scatter=3.6, pe=0.55, peo=8.0, sem=80.0, remote=2600.0, first=2000.0,
               ghold=300.0, dma=1300.0, bw=280.0, dhold=100.0, link=50.0)
CHUNKS = {"W": [(0, 256)], "H": [(0, 128), (128, 256)], "A": [(0, 64), (128, 192), (64, 128), (192, 256)],
          "Y": [(0, 128), (128, 192), (192, 256)], "-": []}
ORDER = """10A 00- 20H 11H 01- 30H 21W  12W 40W 31W 22W 02- 50W  13W 41W 32W 23W 03- 51W  14W 42W 33W 24W 52W 04-
           15W 43W 34W 25H 53H  44H 35H 54H 45H 55Y"""

TUNE = dict(
    seq=[(int(_w[0]), int(_w[1]), CHUNKS[_w[2]]) for _w in ORDER.split()],
    loads=[(0, 256), (256, 1024), (1024, 1792), (1792, 2048)], sa=2,
    pieces=[(0, 256, 0), (256, 1024, 256), (1024, 1792, 256), (1792, 2048, 128)],
    turn_s=(1, 2, 3, 4), wide=(3, 4, 5), on_s=("z1s",),
    pools=[0, 1024, 3072, 2048, 2048, 2048], pool=768,
    now=[1024, 512, 2048, 2048], behind=512,
    margin=300.0, ahead=300.0, skew=-50.0, rounds=2, damp=0.5)


def units(name, t, a, b, w=8):
    return [(name, t, u) for u in range(a // w, (b + w - 1) // w)]


def make_ops(tune):
    A, AF = AluOpType, ActivationFunctionType
    ops, wrote, read, pairs = [], {}, {}, []
    count = dict(msg=0, dma=0, tile=0, bank=0, copy=(-1, WIDE), stop=WIDE)

    def add(eng, cost, r, w, emit, fixed=False, sem=None, to=0):
        deps = set()
        for x in r:
            if x in wrote:
                deps.add(wrote[x])
        for x in w:
            if x in wrote:
                deps.add(wrote[x])
            deps.update(read.get(x, ()))
        me = len(ops)
        for x in r:
            read.setdefault(x, []).append(me)
        for x in w:
            wrote[x] = me
            read[x] = []
        ops.append(dict(eng=eng, cost=cost, deps=sorted(deps), emit=emit, fixed=fixed, sem=sem, to=to))
        return me

    def dma(nbytes, r, w, emit):
        add("y", ("dma", nbytes), r, w, emit, sem="d%d" % count["dma"])
        count["dma"] += 1

    def send(to, nbytes, r, w, sides):
        n = count["msg"]
        add("g", ("remote", nbytes), r, [("left", n)], sides, sem="m%d" % n, to=to)
        add("", ("lands", nbytes), [("left", n)], w, None, sem="m%d" % n, to=to)
        count["msg"] += 1
        pooled(len(ops) - 2)
        more(tune["behind"], [("left", n)])

    def send_lanes(to, src, dst, t, u, a, b):
        send(to, 256 * (b - a), units(src, t, a, b), units(dst, u, a, b), lambda T: (lane(T, dst, u, a, b), lane(T, src, t, a, b)))

    def pooled(after):
        t, a = count["copy"]
        b = count["stop"]
        c = max(a, b - tune["pool"], WIDE - tune["pools"][t + 1])
        if c < b:
            i = convert(b - c, tabs(t, c, b), tabs(t + 1, c, b), lambda T: (tab(T, t + 1)[:, c:b], tab(T, t)[:, c:b]))
            if after is not None:
                ops[i]["deps"].append(after)
                ops[i]["soft"] = after
            count["stop"] = c

    def more(n, behind):
        t, a = count["copy"]
        b = min(a + n, count["stop"] if n == WIDE else min(count["stop"], WIDE - tune["pools"][t + 1]))
        if b > a:
            copy(t, a, b, behind)
            count["copy"] = (t, b)

    def copy(t, a, b, behind=()):
        dma(512 * (b - a), tabs(t, a, b) + list(behind), tabs(t + 1, a, b),
            lambda q, T: q.dma_start(tab(T, t + 1)[:, a:b], tab(T, t)[:, a:b]))

    def last_column(t):
        dma(8192, tabs(t, 0, 1), [("end", t)], lambda q, T: q.dma_start(tab(T, t)[:, WIDE:WIDE + 1], tab(T, t)[:, 0:1]))

    def lane(T, name, t, a, b):
        return T[name][:, LANES * t + a:LANES * t + b]

    def tabs(t, a=0, b=WIDE):
        return units("tab", t, a, b, 128)

    def tab(T, t):
        return T["tab%d" % t]

    def bank():
        count["bank"] += 1
        return "ps%d" % ((count["bank"] - 1) % NBANK)

    def parts(a, b):
        return [(h, max(a, 128 * h), min(b, 128 * h + 128)) for h in range(a // 128, (b + 127) // 128)]

    def const(q, T, out, n, which, start, stop=False):
        rows = SUMS[which][1]
        return q.matmul(out, T.cut[0:rows, 128 * which:128 * which + 128], T.ones[0:rows, 0:n], start, stop)

    def scaled(eng, n, r, w, sides, plus):
        if eng == "v":
            add("v", ("el", n), r, w, lambda q, T: q.tensor_scalar(sides(T)[0], sides(T)[1], plus, None, A.add))
        else:
            add("s", ("el", n), r, w, lambda q, T: q.activation(sides(T)[0], sides(T)[1], AF.Identity, bias=plus))

    def convert(n, r, w, sides):
        return add("g", ("gp", n), r, w, lambda q, T: q.affine_select(sides(T)[0], sides(T)[1], [[0, n]], A.is_ge, 0.0, 0, 0))

    for n, (a, b) in enumerate(tune["loads"]):
        dma(512 * (b - a), [], units("pm", 0, a, b, 128), lambda q, T, a=a, b=b: q.dma_start(T.pmi[:, a:b], T.pm[:, a:b]))
        if n == tune["sa"]:
            dma(512 * LANES, [], ["si"], lambda q, T: q.dma_start(T.si[:], T.sa[:]))
    add("v", ("el", 128), [], ["ones"], lambda q, T: q.memset(T.ones[:, 0:256], 1.0))
    add("v", ("el", 896), [], ["many"], lambda q, T: q.memset(T.ones[:, 256:2048], 1.0))
    add("v", ("el", 16), [], ["pad"], lambda q, T: q.memset(T.dm[:, 0:16], 0.0))
    for n, (x, rows) in enumerate(SUMS[:5]):
        add("s", ("el", 128), ["ones"], [("cut", n)],
            lambda q, T, n=n, x=x / rows: q.activation(T.cut[:, 128 * n:128 * n + 128], T.ones[:, 0:128], AF.Identity, scale=x))
    add("g", ("gp", 16), [], ["x1"], lambda q, T: q.iota(T.x1[:], [[0, 16]], 0, 16))
    add("g", ("gp", 256), ["ones"], ["eye"],
        lambda q, T: q.affine_select(T.eye[:], T.ones[:, 0:256], [[0, 2], [-1, 128]], A.is_equal, 0.0, 0, 1))
    add("g", ("gp", 16), ["eye"], ["x2"], lambda q, T: q.iota(T.x2[:], [[256, 16]], 0, 0))
    ops[-1]["soft"] = len(ops) - 2
    add("g", ("gp", 2048), ["ones", "many"], ["dm"],
        lambda q, T: q.affine_select(T.dm[:, 16:2064], T.ones[:], [[-1, 16], [-512, 8], [-31, 16]], A.is_equal, 0.0, 0, 32))
    add("v", ("el", 16), ["x1"], ["x3"], lambda q, T: q.tensor_scalar(T.x3[:], T.x1[:], 255, None, A.bitwise_and))
    add("v", ("el", 32), ["x3", "x2"], ["x4"], lambda q, T: q.tensor_tensor(T.x4[:], T.x3[:], T.x2[:], A.add))
    add("v", ("el", 16), ["x4"], ["base"], lambda q, T: q.tensor_scalar(T.base[:], T.x4[:], 7.5, None, A.add))
    add("s", ("el", 256), ["eye"], ["neg"], lambda q, T: q.activation(T.neg[:], T.eye[:], AF.Identity, scale=-1.0))
    add("v", ("el", 256), ["eye"], ["rot"], lambda q, T: q.tensor_tensor(T.rot[:, 0:255], T.eye[:, 0:255], T.eye[:, 1:256], A.add))
    add("v", ("el", 32), ["eye"], ["rot"], lambda q, T: q.tensor_tensor(T.rot[:, 15:256:16], T.eye[:, 15:256:16], T.eye[:, 0:256:16], A.add))
    convert(128, ["rot", "dm"], ["rot32"], lambda T: (T.eye32[:, 256:384], T.rot[:, 0:128]))
    scaled("v", LANES, ["si"], units("sl", 0, 0, LANES), lambda T: (lane(T, "sl", 0, 0, LANES), T.si[:]), -MID)

    def late_constants(t):
        r = ["eye", "neg", ("md", t)]
        add("g", ("gp", 128), r, [("cut", 5)],
            lambda q, T: q.affine_select(T.cut[:, 640:768], T.ones[:, 0:128], [[0, 128]], A.is_gt, SUMS[5][0] / SUMS[5][1], 0, 0))
        convert(128, r, ["eye32"], lambda T: (T.eye32[:, 0:128], T.eye[:, 0:128]))
        convert(128, r, ["neg32"], lambda T: (T.eye32[:, 128:256], T.neg[:, 0:128]))

    def index1(t, a, b, ps):
        n, o, turned = b - a, 112 if t else 0, t - 1 in tune["turn_s"]
        wide = t in tune["wide"]
        if wide:
            convert(n, tabs(t, 16 * a, 16 * b), units("pn", t, a, b), lambda T: (lane(T, "pw", t, a, b), tab(T, t)[:, 16 * a + t:16 * b:16]))
        else:
            scaled("s", n, tabs(t, 16 * a, 16 * b), units("pn", t, a, b),
                   lambda T: (lane(T, "pn", t, a, b), tab(T, t)[:, 16 * a + t:16 * b:16]), -MID)

        def sums(q, T):
            def both(eye, eye32, stop):
                if turned:
                    for h, c, d in parts(a, b):
                        w = SW * (2 * t + h)
                        q.matmul(T[ps][:, c - a:d - a], T.sv[:, w:w + 128], eye[:, c - 128 * h:d - 128 * h], False, False)
                else:
                    q.matmul(T[ps][:, 0:n], eye[:, o:o + 128], lane(T, "sl", t, a, b), False, False)
                if wide:
                    return q.matmul(T[ps][:, 0:n], eye32, lane(T, "pw", t, a, b), False, stop)
                return q.matmul(T[ps][:, 0:n], eye[:, 0:128], lane(T, "pn", t, a, b), False, stop)
            const(q, T, T[ps][:, 0:n], n, 5 if wide else 0, True)
            both(T.neg, T.eye32[:, 128:256], False)
            const(q, T, T[ps][:, 0:n], n, 1, False)
            const(q, T, T[ps][:, 0:n], n, 2, False)
            return both(T.eye, T.eye32[:, 0:128], True)
        r = [("sv", t, h) for h, _, _ in parts(a, b)] if turned else units("sl", t, a, b)
        r += ["eye", "neg", "ones", ("cut", 0), ("cut", 1), ("cut", 2)] + (["eye32", "neg32", ("cut", 5)] if wide else [])
        add("p", ("mm", [n] * (13 if wide else 7)), r + units("pn", t, a, b), [ps], sums)
        scaled("s" if "o1" in tune["on_s"] and t else "v", n, [], [ps] + units("o1", t, a, b),
               lambda T: (lane(T, "o1", t, a, b), T[ps][:, 0:n]), MID if wide else 0.0)

    for a, b, v in tune["pieces"]:
        pmr, c = units("pm", 0, a, b, 128), a + v
        if c < b:
            add("s", ("el", b - c), pmr, [("hi", a)],
                lambda q, T, c=c, b=b: q.activation(T.hi[:, c:b], T.pmi[:, c:b], AF.Identity,
                                                    bias=-(2047.0 + 2047.5 / WIDE), scale=1.0 / WIDE))
            add("s", ("el", b - c), [("hi", a)], tabs(0, HALF + c, HALF + b),
                lambda q, T, c=c, b=b: q.activation(T.tab0[:, HALF + c:HALF + b], T.hi[:, c:b], AF.Identity, bias=2047.0))
        add("v", ("el", b - a), pmr, tabs(0, a, b),
            lambda q, T, a=a, b=b: q.tensor_scalar(T.tab0[:, a:b], T.pmi[:, a:b], WIDE - 1, None, A.bitwise_and))
        if v:
            add("v", ("el", v), pmr, tabs(0, HALF + a, HALF + c),
                lambda q, T, a=a, c=c: q.tensor_scalar(T.tab0[:, HALF + a:HALF + c], T.pmi[:, a:c], 12, None, A.logical_shift_right))
        for c, d in tune["seq"][0][2]:
            if a < max(16 * (y - 128 * h) for h, _, y in parts(c, d)) <= b:
                index1(0, c, d, bank())
        if b in (1024, 2048):
            for x in (0, HALF):
                c = x + b - 1024 + (max(0, min(1024, tune["pools"][1] - x // 2)) if b == 1024 else 0)
                if c > x + b - 1024:
                    convert(c - x, ["dm"] + tabs(0, x, c), tabs(1, x, c), lambda T, x=x, c=c: (T.tab1[:, x:c], T.tab0[:, x:c]))
                if c < x + b:
                    copy(0, c, x + b)
    last_column(0)

    def gather(k, t, a, b, tile, whole):
        last, n = t == STEPS - 1, b - a
        s0 = WIDE * tile
        off, wide = "o%d" % k, WIDE + 1 if k == 4 else WIDE
        r = tabs(t) + ([("end", t)] if k == 4 else []) + units(off, t, a, b)
        got = units("gv", tile, a, b) + units("gs", tile, a, b)
        cut = [a]

        def by_vector(q, T):
            c = cut[0]
            return q.tensor_scalar(T.gg[:, s0 + 16 * a:s0 + 16 * c], tab(T, t)[:, 0:wide].indirect(lane(T, off, t, a, c)), -MID, None, A.add)

        def by_scalar(q, T):
            c = cut[0]
            return q.activation(T.gg[:, s0 + 16 * c:s0 + 16 * b], tab(T, t)[:, 0:wide].indirect(lane(T, off, t, c, b)), AF.Identity, bias=-MID)
        x = add("v", ("gather", 8 * n), r, [], by_vector, fixed=True)
        y = add("s", ("gather", 8 * n), r, [], by_scalar, fixed=True)
        for z in (x, y):
            ops[z]["deps"] = sorted(set(ops[z]["deps"]).union(*[read.get(u, ()) for u in got]))
        for u in got:
            wrote[u], read[u] = x if u[0] == "gv" else y, []
        pairs.append((x, y, a, b, cut))
        ps = bank()

        def offsets(name, plus, ps=ps):
            scaled("s" if name in tune["on_s"] else "v", n, [], [ps] + units(name, t, a, b),
                   lambda T: (lane(T, name, t, a, b), T[ps][:, 0:n]), plus)

        def keep(name):
            scaled("s", n, [], [ps] + units(name, t, a, b), lambda T: (lane(T, name, t, a, b), T[ps][:, 0:n]), 0.0)

        if k == 1 and t in tune["turn_s"]:
            halves = [h for h, _, _ in parts(a, b)]
            h0, h1 = halves[0], halves[-1] + 1

            def turn(q, T):
                for h in halves:
                    for j in range(16):
                        w = SW * (h - h0)
                        m = q.matmul(T[ps][:, w + j:w + SW:16], T.gg[:, s0 + HALF * h + j:s0 + HALF * (h + 1):16],
                                     T.eye[:, 112 + j:256:16], True, True)
                return m
            add("p", ("mm", [64] * 16 * len(halves)), ["eye"] + got, [ps], turn)
            w0, w1, mine = SW * (2 * t + h0), SW * (2 * t + h1), [("su", t, h) for h in halves]
            scaled("s", w1 - w0, [], [ps] + mine, lambda T: (T.su[:, w0:w1], T[ps][:, 0:w1 - w0]), 0.0)
            send(1, 256 * (w1 - w0), mine, [("sv", t + 1, h) for h in halves],
                 lambda T: (T.sv[:, w0 + 2 * SW:w1 + 2 * SW], T.su[:, w0:w1]))
            back = bank()

            def turn_back(q, T):
                for h in halves:
                    w = SW * (2 * t + h) + 16
                    m = q.matmul(T[back][:, 128 * (h - h0):128 * (h - h0 + 1)], T.su[:, w:w + 128], T.eye[:, 0:128], True, True)
                return m
            add("p", ("mm", [128] * len(halves)), ["eye"] + mine, [back], turn_back)
            offsets("o2", MID, back)
        else:
            def pick(q, T):
                for j in range(16):
                    m = q.matmul(T[ps][:, 0:n], T.dm[:, 16 + 128 * j:144 + 128 * j], T.gg[:, s0 + 16 * a + j:s0 + 16 * b:16],
                                 j == 0, j == 15 and k != 4)
                return m
            add("p", ("mm", [n] * 16), ["dm"] + got, [ps], pick)
            if k == 1:
                offsets("o2", MID)
                if not last:
                    keep("s16")
                    send_lanes(1, "s16", "sl", t, t + 1, a, b)
                else:
                    convert(n, units("o2", t, a, b), units("s16", t, a, b), lambda T: (T.yo[:, a:b], lane(T, "o2", t, a, b)))
                    if whole:
                        dma(512 * LANES, units("s16", t, 0, LANES), [], lambda q, T: q.dma_start(T.ys[:], T.yo[:, 0:LANES]))
            elif k == 2:
                offsets("z1s", MID)
                send_lanes(1, "z1s", "o3", t, t, a, b)
            elif k == 3:
                offsets("z2s", MID + 1.0)
                send_lanes(-1, "z2s", "o4", t, t, a, b)
            elif k == 4:
                index5(t, a, b, ps)
            elif not last:
                keep("t16")
                send_lanes(1, "t16", "tl", t, t + 1, a, b)
            else:
                scaled("s", n, [], [ps] + units("t16", t, a, b), lambda T: (T.yo[:, LANES + a:LANES + b], T[ps][:, 0:n]), MID)
                dma(512 * n, units("t16", t, a, b), [], lambda q, T: q.dma_start(T.yt[:, a:b], T.yo[:, LANES + a:LANES + b]))
        if k == 1 and whole and not last:
            places(t, s0, tile)

    def index5(t, a, b, ps):
        n = b - a

        def sums(q, T):
            if t:
                q.matmul(T[ps][:, 0:n], T.rot[:, 112:240], lane(T, "tl", t, a, b), False, False)
            else:
                q.matmul(T[ps][:, 0:n], T.eye32[:, 256:384], T.tw[:, a:b], False, False)
            return const(q, T, T[ps][:, 0:n], n, 3, False, True)
        add("p", ("mm", [max(n, 64) * (2 if t else 5)]), units("tl", t, a, b) + ["rot", "rot32", ("cut", 3)], [ps], sums)
        add("s", ("el", n), [], [ps, ("m5", t, a)],
            lambda q, T: q.activation(lane(T, "m5", t, a, b), T[ps][:, 0:n], AF.Identity, bias=2047.5, scale=-1.0))
        add("v", ("el", n), [("m5", t, a)], [ps] + units("o5", t, a, b),
            lambda q, T: q.tensor_tensor(lane(T, "o5", t, a, b), T[ps][:, 0:n], lane(T, "m5", t, a, b), A.add))

    def places(t, s0, tile):
        def spread(q, T):
            for j in range(16):
                q.matmul(T.ps6[:, 0:16], T.dm[:, 16 - j:144 - j], T.gg[:, s0 + 16 * j:s0 + WIDE:256], j == 0, False)
            return const(q, T, T.ps6[:, 0:16], 16, 4, False, True)
        add("p", ("mm", [16] * 17), ["dm", "pad", ("cut", 4)] + units("gv", tile, 0, LANES) + units("gs", tile, 0, LANES), ["ps6"], spread)
        add("v", ("el", 16), ["base"], ["ps6", ("md", t)],
            lambda q, T: q.tensor_tensor(T.md[:, 16 * t:16 * t + 16], T.base[:], T.ps6[:, 0:16], A.subtract))
        add("v", ("el", 16), [("md", t)], ["ps6", ("li", t)],
            lambda q, T: q.tensor_tensor(T.li[:, 16 * t:16 * t + 16], T.ps6[:, 0:16], T.md[:, 16 * t:16 * t + 16], A.add))

    def swap(t, chunks):
        more(WIDE, [])
        if t + 1 == min(tune["wide"]):
            late_constants(t)
        add("v", ("scatter", LANES), tabs(t) + [("li", t)], tabs(t + 1),
            lambda q, T: q.tensor_copy(tab(T, t + 1)[:, 0:WIDE].indirect(T.li[:, 16 * t:16 * t + 16]), tab(T, t)[:, t:WIDE:16]))
        add("s", ("gather", LANES), tabs(t) + [("li", t)], tabs(t + 1),
            lambda q, T: q.activation(tab(T, t + 1)[:, t:WIDE:16], tab(T, t)[:, 0:WIDE].indirect(T.li[:, 16 * t:16 * t + 16]), AF.Copy))
        for a, b in chunks:
            index1(t + 1, a, b, "ps6")
        if t == 0:
            dma(512 * LANES, [("left", 0)], ["ti"], lambda q, T: q.dma_start(T.ti[:], T.ta[:]))
            convert(LANES, ["ti"], units("tl", 0, 0, LANES), lambda T: (T.tw[:], T.ti[:]))
        last_column(t + 1)
        if t < STEPS - 2:
            count["copy"], count["stop"] = (t + 1, 0), WIDE
            pooled(None)
            more(tune["now"][t], [])

    for k, t, chunks in tune["seq"]:
        if k == 0:
            swap(t, [c for j, u, c in tune["seq"] if (j, u) == (1, t + 1)][0])
            continue
        tile = count["tile"] % NG
        count["tile"] += 1
        for a, b in chunks:
            gather(k, t, a, b, tile, (a, b) == chunks[-1])
    return ops, pairs


def spans(op, M, state, start):
    kind, n = op["cost"]
    if kind == "dma":
        state["dma"] = max(start + M["dma"] / 2, state.get("dma", 0.0)) + n / M["bw"]
        return start + M["dhold"], state["dma"] + M["dma"] / 2
    if kind == "remote":
        extra = 0.0 if state.get("sent") else M["first"]
        state["sent"] = True
        state["dma"] = max(start + extra + M["remote"] / 2, state.get("dma", 0.0)) + n / M["link"]
        return start + M["ghold"] + extra, state["dma"]
    if kind == "lands":
        return 0.0, start + M["remote"] / 2
    if kind == "mm":
        d = sum(max(64, x) * M["pe"] + M["peo"] for x in n)
    elif kind == "gp":
        d = 170.0 + 2 * n * M["cyc"]
    else:
        rate = 1.0 if kind == "el" else M[kind]
        d = (55.0 if op["eng"] == "v" else 70.0) + max(64, n * rate) * M["cyc"]
    return start + d, start + d


def order_ops(ops, pairs, tune, M, skew):
    n = len(ops)
    left = [len(o["deps"]) for o in ops]
    after = [[] for _ in ops]
    for i, o in enumerate(ops):
        for d in o["deps"]:
            after[d].append(i)
    need = [len(pairs)] * n
    for m, p in enumerate(pairs):
        need[p[0]] = need[p[1]] = m
    for i in reversed(range(n)):
        for d in ops[i]["deps"]:
            if not ops[d]["fixed"]:
                need[d] = min(need[d], need[i])
    for i in range(len(tune["loads"]) + 1):
        need[i] = -1
    free = {e: 0.0 for e in ["v", "s", "p", "g", "y", ""]}
    end, state, order, idle = [0.0] * n, {}, [], []
    due, ready = {i: 0.0 for i in range(n) if not left[i]}, [0.0] * n
    column, head, busy = 16 * M["gather"] * M["cyc"], 0, {"v": 0.0, "s": 0.0}

    def slack(o, d):
        return tune["margin"] if o["eng"] in "vs" and ops[d]["eng"] not in "vs" else 0.0

    def run(i):
        e = ops[i]["eng"]
        free[e], end[i] = spans(ops[i], M, state, max(free[e], ready[i]))
        order.append(i)
        del due[i]
        for j in after[i]:
            left[j] -= 1
            if not left[j]:
                hard = [d for d in ops[j]["deps"] if d != ops[j].get("soft")]
                ready[j] = max([end[d] + M["sem"] for d in hard], default=0.0)
                due[j] = max([end[d] + M["sem"] + slack(ops[j], d) for d in hard], default=0.0)
    while due:
        best = min(((max(free[ops[i]["eng"]], r), need[i], i) for i, r in due.items() if not ops[i]["fixed"]), default=None)
        if head < len(pairs):
            x, y, a, b, cut = pairs[head]
            if x in due and y in due:
                sv, ss = max(free["v"], ready[x]), max(free["s"], ready[y])
                if best is None or max(sv, ss) + tune["ahead"] < best[0]:
                    idle.append(ss - busy["s"] - sv + busy["v"])
                    v = 2 * round(((b - a) / 2 + (ss - sv - skew[head]) / (2 * column)) / 2)
                    cut[0] = a + min(max(v, 2), b - a - 2)
                    ops[x]["cost"], ops[y]["cost"] = ("gather", 16 * (cut[0] - a)), ("gather", 16 * (b - cut[0]))
                    run(x)
                    run(y)
                    busy["v"], busy["s"] = free["v"], free["s"]
                    head += 1
                    continue
        o = ops[best[2]]
        if o["eng"] in busy:
            busy[o["eng"]] += spans(o, M, {}, 0.0)[0]
        run(best[2])
    return order, idle[1:] + [0.0]


PLAN = {}


def plan():
    if not PLAN:
        ops, pairs = make_ops(TUNE)
        skew = [0.0] * len(pairs)
        for _ in range(TUNE["rounds"] + 1):
            order, idle = order_ops(ops, pairs, TUNE, NOMINAL, skew)
            skew = [x + TUNE["damp"] * (y + TUNE["skew"]) for x, y in zip(skew, idle)]
        PLAN["ops"], PLAN["order"] = ops, order
    return PLAN["ops"], PLAN["order"]


def rank_program(g, core, T, topo):
    rank = T.rank_of(core)
    if rank is None:
        return
    ops, order = plan()
    cores = list(T.cores)
    queue = {"v": g.vector, "s": g.scalar, "p": g.tensor, "g": g, "y": g.sync}
    mark, know, total = {}, {e: {} for e in queue}, {}
    for i in order:
        o = ops[i]
        if not o["eng"]:
            mark[i] = (o["sem"], len(topo.engines(cores[(rank - o["to"]) % len(cores)], core)), {})
            continue
        e, q = o["eng"], queue[o["eng"]]
        need = {}
        for d in o["deps"]:
            s, val, _ = mark[d]
            if (e == "p" and s == "p") or d == o.get("soft"):
                continue
            if need.get(s, (0, None))[0] < val:
                need[s] = (val, d)
        for s, (val, d) in sorted(need.items(), key=lambda x: -x[1][1]):
            if know[e].get(s, 0) < val:
                q.wait_ge(T.sem[s], val)
                know[e][s] = val
                for s2, v2 in mark[d][2].items():
                    know[e][s2] = max(know[e].get(s2, 0), v2)
        if o["to"]:
            other = cores[(rank + o["to"]) % len(cores)]
            rid, pid, _ = topo.addr(other)
            out, src = o["emit"](T)
            g.remote_dma(out, src, T.sem[o["sem"]], T.sem["l" + o["sem"]], pid, rid, topo.mask(core, other))
            total["l" + o["sem"]] = len(topo.engines(core, other))
            mark[i] = ("l" + o["sem"], total["l" + o["sem"]], {})
        elif o["sem"]:
            o["emit"](q, T).then_inc(T.sem[o["sem"]], 16)
            total[o["sem"]] = 16
            mark[i] = (o["sem"], 16, dict(know[e]))
        else:
            o["emit"](q, T).then_inc(T.sem[e], 1)
            total[e] = total.get(e, 0) + 1
            mark[i] = (e, total[e], dict(know[e]))
    for s, val in total.items():
        if know["y"].get(s, 0) < val:
            g.sync.wait_ge(T.sem[s], val)
